import numpy as np, ml_dtypes
CORES = [24,25,26,27,28,29,30,31]
N = 8
import mx_ref
BF = ml_dtypes.bfloat16
def gentries(a):
    return np.ascontiguousarray(a.reshape(8, 16, -1).transpose(0, 2, 1)).reshape(8, -1)
def gtable(e):
    e = np.asarray(e); return np.ascontiguousarray(e.reshape(8, -1, 16).transpose(0, 2, 1)).reshape(128, -1).astype(np.int32)
def gcols(t, e):
    v = np.concatenate([t.reshape(8, 16, -1, 4), np.zeros((8, 16, 1, 4), BF)], axis=2)
    return np.ascontiguousarray(np.stack([v[g][:, e[g]] for g in range(8)])).reshape(128, -1)
def tile(rs):
    return np.stack(rs, axis=2).reshape(128, -1).astype(BF)
def pick(q, e):
    c = np.concatenate([q[0].reshape(128, -1, 4), np.zeros((128, 1, 4), np.uint8)], axis=1); s = np.concatenate([q[1], np.ones((16, 1), np.uint8)], axis=1)
    return (np.ascontiguousarray(c[:, e].reshape(128, -1)), np.ascontiguousarray(s[:, e]))
def join(*qs):
    return (np.concatenate([q[0] for q in qs], axis=1), np.concatenate([q[1] for q in qs], axis=1))
def put(q, e, v):
    c, s = q[0].reshape(128, -1, 4).copy(), q[1].copy(); c[:, e] = v[0].reshape(128, -1, 4); s[:, e] = v[1]
    return (c.reshape(128, -1), s)
def pk(c, s):
    return (np.ascontiguousarray(c), mx_ref.live(s))
def emit(q):
    return q[0], q[1]
def packed(v, rng):
    q = [mx_ref.quantize(np.ascontiguousarray(v[r])) for r in range(N)]
    return np.stack([a for a, b in q]), np.stack([mx_ref.plane(b, rng) for a, b in q])
def f(rng, *shape):
    return mx_ref.flush((rng.standard_normal(shape, dtype=np.float32) * np.exp2(rng.integers(-2, 3, shape[:-1] + (1,)))).astype(BF))
def wide(rng, *shape, cols=0):
    v = rng.standard_normal(shape, dtype=np.float32) * np.exp2(rng.integers(-12, 13, shape)).astype(np.float32)
    if cols: v *= np.repeat(np.exp2(rng.integers(-cols, cols + 1, shape[:-2] + (1, shape[-1] // 4))) * (rng.random(shape[:-2] + (1, shape[-1] // 4)) > 0.0625), 4, axis=-1).astype(np.float32)
    return mx_ref.flush(v.astype(BF))
C, R = 416, 2
def partners(rng, n):
    e = np.tile(np.arange(C), (N, 8, 1))
    p = rng.permuted(e, axis=2)
    k, m = p[:, :, :n], p[:, :, n:2 * n]
    np.put_along_axis(e, k, m, axis=2)
    np.put_along_axis(e, m, k, axis=2)
    return e
def stored(e):
    return np.stack([gtable(e[r]) for r in range(N)])
def layers(rng, v, w):
    (a, b), (c, d) = packed(v, rng), packed(w, rng)
    return {"vc": a, "vs": b, "wc": c, "ws": d}
def units(rng, kv, kw):
    w = np.zeros((N, 128, 4, 128, 4), np.float32)
    i = np.arange(128)
    for b in range(4): w[:, i, b, i, b] = 1
    w = w.reshape(N, 128, 2048)
    return layers(rng, *[(w * np.reshape(k, (N, 1, 1)).astype(np.float32) + np.float32(0.0)).astype(BF) for k in (kv, kw)])
def moves_alone(rng):
    k = rng.permutation(N) % 2 * 32.0
    return units(rng, k, 32.0 - k)
def setup_inputs(rng):
    return {"x": np.array(f(rng, N, 128, 4 * C)), "pr": stored(partners(rng, int(rng.integers(3 * C // 8, C // 2 + 1)))), "u": np.array(f(rng, N, 128, 512)), "a": np.array(f(rng, N, 128, 512)), **layers(rng, f(rng, N, 128, 2048), f(rng, N, 128, 2048))}
def setup_inputs_rest(rng):
    d = setup_inputs(rng)
    e = partners(rng, C // 2)
    o = rng.permutation(N)
    d["x"][o[0]] = 0
    e[o[1]] = np.arange(C)
    d["pr"] = stored(e)
    return d
def setup_inputs_near(rng):
    d = setup_inputs(rng)
    e = partners(rng, C // 2)
    j = np.arange(C)
    n = np.cumsum(e > j, axis=2) - 1
    n = np.take_along_axis(n, np.minimum(e, j), axis=2)
    flip = np.take_along_axis(rng.integers(0, 2, (N, 8, C // 2)), n, axis=2) > 0
    h = np.take_along_axis(rng.integers(-3, 4, (N, 8, C // 2)), n, axis=2)
    first = (e > j) ^ flip
    kind = n % 9
    plus = np.where(kind == 7, True, np.where(kind == 8, False, first))
    m = np.where(first, h, kind - 3 - h)
    size = np.exp2(np.arange(4) - 23.0)
    x = np.zeros((N, 8, 16, C, 4), np.float32)
    x[:, :, 0, :, 0] = plus
    x[:, :, 1, :, 0] = ~plus
    x[:, :, 2:8] = rng.integers(4, 8, (N, 8, 6, C, 4)) * 0.125
    x[:, :, 8] = ((np.maximum(m, 0)[..., None] >> np.arange(4)) & 1) * size
    x[:, :, 9] = ((np.maximum(-m, 0)[..., None] >> np.arange(4)) & 1) * size
    x[:, :, 10:] = rng.integers(4, 8, (N, 8, 6, C, 4)) * 2.0 ** -20
    u = np.zeros((N, 128, 8, 4), np.float32)
    for g in range(8):
        u[:, 16 * g, g, 0] = 1
        u[:, 16 * g + 1, g, 0] = -1
        u[:, 16 * g + 8, g] = 1
        u[:, 16 * g + 9, g] = -1
    z = rng.permutation(N) % 3 - 1.0
    x = x * np.exp2(7 * z).reshape(N, 1, 1, 1, 1)
    u = u * np.exp2(30 * z).reshape(N, 1, 1, 1) + 0.0
    d["x"] = x.astype(np.float32).reshape(N, 128, 4 * C).astype(BF)
    d["pr"] = stored(e)
    d["u"].reshape(N, 128, 128, 4)[:, :, ::16] = u.astype(np.float32).astype(BF)
    return {**d, **moves_alone(rng)}
def setup_inputs_huge(rng):
    d = setup_inputs(rng)
    x = 2.0 ** 30 * (0.6 + 0.4 * rng.random((N, 128, C, 4)))
    s = np.stack([rng.permutation(8) % 2 * 2.0 - 1.0 for r in range(N)])
    o = rng.permutation(N)
    s[o[0]] = 1
    s[o[1]] = -1
    g = np.ones((N, 128, 8)) * s[:, None, :]
    for r in o[2::2]:
        g[r, 64:] *= -1
        c = rng.permutation(C) % 2 == 0
        x[r, :64] *= np.where(c, 1.0, 2.0 ** -20)[None, :, None]
        x[r, 64:] *= np.where(c, 2.0 ** -20, 1.0)[None, :, None]
    u = 2.0 ** 30 * (1 - 0.25 * rng.random((N, 128, 8, 4))) * g[..., None]
    d["x"] = x.astype(np.float32).reshape(N, 128, 4 * C).astype(BF)
    d["pr"] = stored(partners(rng, C // 2))
    d["u"].reshape(N, 128, 128, 4)[:, :, ::16] = u.astype(np.float32).astype(BF)
    return {**d, **moves_alone(rng)}
def setup_inputs_flip(rng):
    d = setup_inputs(rng)
    x = (1 + rng.random((N, 128, C, 4))) * np.exp2(rng.integers(24, 29, (N, 1, C, 1)))
    u = (1 + rng.random((N, 128, 8, 4))) * (rng.permutation(N) % 2 * 2.0 - 1.0).reshape(N, 1, 1, 1)
    d["x"] = x.astype(np.float32).reshape(N, 128, 4 * C).astype(BF)
    d["pr"] = stored(partners(rng, C // 2))
    d["u"].reshape(N, 128, 128, 4)[:, :, ::16] = u.astype(np.float32).astype(BF)
    return {**d, **units(rng, np.full(N, -32.0), np.full(N, -32.0))}
def setup_inputs_spread(rng):
    d = setup_inputs(rng)
    d["x"] = wide(rng, N, 128, 4 * C, cols=6)
    return d
def check_inputs(d):
    b = []
    for k in ("x", "u", "a"):
        v = np.abs(d[k].astype(np.float32))
        if not (np.isfinite(v).all() and ((v == 0) | (v >= 2.0 ** -30) & (v <= 2.0 ** 30)).all()): b.append("a value of " + k)
    e = np.stack([gentries(p) for p in d["pr"]])
    if ((e < 0) | (e >= C)).any(): b.append("an entry of pr is out of range")
    elif (np.take_along_axis(e, e, axis=2) != np.arange(C)).any(): b.append("a column isn't its partner's partner")
    for k in ("v", "w"):
        c = d[k + "c"] & 127
        s = np.stack([mx_ref.live(p) for p in d[k + "s"]]).astype(int)
        if (c == 127).any(): b.append("a code of " + k + "c isn't a number")
        full = c.reshape(N, 16, 8, 512, 4).any(axis=(2, 4))
        if ((s > 157) | full & (s < 80)).any(): b.append("a scale of " + k + "s is out of range")
    return b
def reference(x, pr, u, a, vc, vs, wc, ws):
    partner = [gentries(pr[r]) for r in range(N)]
    qu = [mx_ref.quantize(u[r]) for r in range(N)]
    lv, lw = [pk(vc[r], vs[r]) for r in range(N)], [pk(wc[r], ws[r]) for r in range(N)]
    four = [np.arange(128 * b, 128 * b + 128) for b in range(4)]
    now = [x[r] for r in range(N)]
    last = np.zeros((N, 8, C), int)
    for t in range(R):
        start = np.arange(C)
        q = []
        for r in range(N):
            s = mx_ref.matmul(qu[r], mx_ref.quantize(now[r]))[::16]
            c = np.where(s + np.take_along_axis(s, partner[r], axis=1) > 0, partner[r], np.arange(C))
            l = [c[0]]
            for g in range(1, 8): l.append(c[g][l[g - 1]])
            l = np.stack(l)
            last[r] = l[:, start]
            q.append(mx_ref.quantize(gcols(now[r], last[r])))
            start = l[7][start]
        now = [tile([np.maximum(mx_ref.matmul(pick(lv[r], k), q[r]), mx_ref.matmul(pick(lw[r], k), q[(r - 1) % N])) * np.float32(0.03125) for k in four]) for r in range(N)]
    y, ol = np.zeros((N, 128, C), np.float32), np.zeros((N, 8, C), np.float32)
    oc, osc = np.zeros((N, 128, 4 * C), np.uint8), np.zeros((N, 16, C), np.uint8)
    for r in range(N):
        z = mx_ref.quantize(now[r])
        y[r] = mx_ref.matmul(mx_ref.quantize(a[r]), z)
        ol[r] = last[r]
        oc[r], osc[r] = emit(z)
    return {"y": y, "ol": ol, "oc": oc, "osc": osc}

@@ -1,0 +1,480 @@
+from concourse.bass import DstId, RemoteDMATransfer
+from concourse.mybir import dt, AluOpType, ActivationFunctionType
+
+C, R, N = 416, 2, 8
+K = C // 16
+KV = 14
+H = 16 * KV
+STEP = 2.0
+WIDE = 512.0
+FX, U8 = "float8_e4m3fn_x4", "uint8"
+
+SCRATCH = {
+    "ut": ("sbuf", [128, 512], "bfloat16"), "at": ("sbuf", [128, 512], "bfloat16"),
+    "qu": ("sbuf", [128, 128], FX), "su": ("sbuf", [128, 128], U8),
+    "qu2": ("sbuf", [128, 128], FX), "su2": ("sbuf", [128, 128], U8),
+    "qa": ("sbuf", [128, 128], FX), "sa": ("sbuf", [128, 128], U8),
+    "vq": ("sbuf", [128, 512], FX), "vp": ("sbuf", [128, 512], U8),
+    "wq": ("sbuf", [128, 512], FX), "wp": ("sbuf", [128, 512], U8),
+    "pri": ("sbuf", [128, K], "int32"), "prf": ("sbuf", [128, K], "float32"), "pr16": ("sbuf", [128, K], "uint16"),
+    "ipi": ("sbuf", [128, 1], "int32"), "ipm": ("sbuf", [128, 1], "int32"), "ipf": ("sbuf", [128, 1], "float32"),
+    "e1": ("sbuf", [128, 1], "float32"), "e2": ("sbuf", [128, 1], "float32"), "e4": ("sbuf", [128, 4], "float32"),
+    "jb": ("sbuf", [128, 32], "float32"), "jw": ("sbuf", [128, 32], "float32"), "uoff": ("sbuf", [128, 8], "uint16"),
+    "dd": ("sbuf", [128, K], "float32"), "jp": ("sbuf", [128, K], "float32"), "tm": ("sbuf", [128, K], "float32"),
+    "jm": ("sbuf", [128, C], "bfloat16"), "a0": ("sbuf", [128, C], "bfloat16"),
+    "a1": ("sbuf", [128, C], "bfloat16"), "a2": ("sbuf", [128, C], "bfloat16"),
+    "idr": ("sbuf", [128, C], "float32"),
+    "sp": ("sbuf", [128, C], "float32"), "sn": ("sbuf", [128, C], "float32"),
+    "vm": ("sbuf", [128, C], "bfloat16"), "sv": ("sbuf", [128, C], "bfloat16"),
+    "cw": ("sbuf", [128, 32], "float32"), "c16": ("sbuf", [128, K], "uint16"),
+    "uu": ("sbuf", [128, 96], "float32"), "wt": ("sbuf", [128, 96], "float32"), "ot": ("sbuf", [128, 96], "uint16"),
+    "r0": ("sbuf", [128, C], "float32"), "r1": ("sbuf", [128, C], "float32"), "r2": ("sbuf", [128, C], "float32"),
+    "r3": ("sbuf", [128, C], "float32"), "r4": ("sbuf", [128, C], "float32"),
+    "sc1": ("sbuf", [128, C], "float32"), "sc2": ("sbuf", [128, 512], "float32"), "sc3": ("sbuf", [128, C], "float32"),
+    "o4": ("sbuf", [128, K], "uint16"), "oy": ("sbuf", [128, 4 * K], "uint16"),
+    "bf": ("sbuf", [128, 48], "float32"), "bw": ("sbuf", [128, 32], "float32"),
+    "b0": ("sbuf", [128, C], "float32"), "b1": ("sbuf", [128, C], "float32"), "ob": ("sbuf", [128, K], "uint16"),
+    "m1": ("sbuf", [128, C], "float32"), "m2": ("sbuf", [128, C], "float32"),
+    "pv": ("sbuf", [128, 4 * C], "float32"), "pw": ("sbuf", [128, 4 * C], "float32"),
+    "ysb": ("sbuf", [128, C], "float32"),
+    "ps": ("psum", [128, 4096], "float32"),
+}
+for _t in range(R + 1):
+    SCRATCH["x%d" % _t] = ("sbuf", [128, 4 * C], "bfloat16")
+    SCRATCH["qx%d" % _t] = ("sbuf", [128, C], FX)
+    SCRATCH["sx%d" % _t] = ("sbuf", [128, C], U8)
+for _t in range(R):
+    SCRATCH["yt%d" % _t] = ("sbuf", [128, 4 * C], "bfloat16")
+    for _n in ("qy", "qz", "qp"):
+        SCRATCH["%s%d" % (_n, _t)] = ("sbuf", [128, C], FX)
+    for _n in ("sy", "sz", "sq"):
+        SCRATCH["%s%d" % (_n, _t)] = ("sbuf", [128, C], U8)
+    SCRATCH["ls%d" % _t] = ("sbuf", [128, K], "uint16")
+    SCRATCH["ll%d" % _t] = ("sbuf", [128, (N - 1) * K], "uint16")
+
+DMAS = ["dx0", "dx1", "du", "dpr", "dvc", "dvs", "dwc", "dws", "da", "doc0", "doc1", "dos0", "dos1", "dos2", "dos3",
+        "dy0", "dy1", "dol"]
+PLAN = {2: "V M", 3: "va va V w M", 4: "va va V v w M", 5: "va va V v v w M", 6: "va va V v v M a w", 7: "va va V v v M a a w"}
+EARLY = [4, 2]
+SEMAPHORES = (["cv", "ca", "ct", "cg", "sent"] + DMAS + ["z%d" % t for t in range(R)]
+              + ["l%d_%d" % (t, q) for t in range(R) for q in range(N - 1)])
+
+
+def list_takers(q, engines):
+    to = [q + 1] + ([0] if q else []) + list(range(N - 1, q + 1, -1))
+    n = [1] * len(to)
+    grown = True
+    while grown:
+        grown = False
+        least = min(n)
+        for i in range(len(to)):
+            if n[i] == least and sum(n) + n[i] <= engines:
+                n[i] *= 2
+                grown = True
+    return list(zip(to, n))
+
+
+def rank_program(g, core, T, topo):
+    r = T.rank_of(core)
+    if r is None:
+        return
+    Op = AluOpType
+    Copy = ActivationFunctionType.Copy
+    queue = {"v": g.vector, "a": g.scalar, "t": g.tensor, "g": g, "s": g.sync}
+    own = {"v": "cv", "a": "ca", "t": "ct", "g": "cg"}
+    count = {s: 0 for s in SEMAPHORES}
+    waited = {s: 0 for s in SEMAPHORES}
+    clock = {e: {} for e in queue}
+    log = {}
+
+    def A(name, c0, c1, step=1, p0=0, p1=128):
+        return (name, c0, c1, step, p0, p1)
+
+    def ap(d):
+        if d[3] == 1:
+            return T[d[0]][d[4]:d[5], d[1]:d[2]]
+        return T[d[0]][d[4]:d[5], d[1]:d[2]:d[3]]
+
+    def meet(a, b):
+        if a[0] == "ps":
+            return a[1] // 512 == b[1] // 512
+        if a[2] <= b[1] or b[2] <= a[1] or a[5] <= b[4] or b[5] <= a[4]:
+            return False
+        if a[3] == b[3] and a[3] > 1 and (a[1] - b[1]) % a[3]:
+            return False
+        return True
+
+    def wait(e, sem, val, seen):
+        if clock[e].get(sem, 0) >= val:
+            return
+        queue[e].wait_ge(T.sem[sem], val)
+        waited[sem] = max(waited[sem], val)
+        for s, v in seen.items():
+            clock[e][s] = max(clock[e].get(s, 0), v)
+
+    def order(e, reads, writes):
+        need = {}
+        for d, w in [(d, False) for d in reads] + [(d, True) for d in writes]:
+            for (o, ow, oe, sem, val, seen) in log.get(d[0], []):
+                if (w or ow or (d[0] == "ps" and oe != e)) and meet(d, o):
+                    if sem not in need or need[sem][0] < val:
+                        need[sem] = (val, seen)
+        for sem, (val, seen) in sorted(need.items(), key=lambda kv: -len(kv[1][1])):
+            wait(e, sem, val, seen)
+
+    def note(e, reads, writes, sem, val):
+        seen = dict(clock[e]) if e else {}
+        seen[sem] = val
+        for d, w in [(d, False) for d in reads] + [(d, True) for d in writes]:
+            log.setdefault(d[0], []).append((d, w, e, sem, val, seen))
+
+    def run(e, call, reads, writes, sem=None):
+        order(e, reads, writes)
+        n = 16 if sem else 1
+        sem = sem or own[e]
+        call().then_inc(T.sem[sem], n)
+        count[sem] += n
+        note(e, reads, writes, sem, count[sem])
+
+    def lands(d, sem, n):
+        count[sem] = n
+        note(None, [], [d], sem, n)
+
+    def b8(d):
+        return ap(d).bitcast(dt.uint8)
+
+    def copy(e, out, in_, scale=None):
+        if e == "a":
+            if scale is None:
+                run(e, lambda: g.scalar.activation(ap(out), ap(in_), Copy), [in_], [out])
+            else:
+                run(e, lambda: g.scalar.activation(ap(out), ap(in_), Copy, scale=scale), [in_], [out])
+        elif scale is None:
+            run(e, lambda: g.vector.tensor_copy(ap(out), ap(in_)), [in_], [out])
+        else:
+            run(e, lambda: g.vector.tensor_scalar(ap(out), ap(in_), scale, None, Op.mult), [in_], [out])
+
+    def gather(e, out, win, off, scale=None):
+        if e == "a":
+            if scale is None:
+                run(e, lambda: g.scalar.activation(ap(out), ap(win).indirect(ap(off)), Copy), [win, off], [out])
+            else:
+                run(e, lambda: g.scalar.activation(ap(out), ap(win).indirect(ap(off)), Copy, scale=scale), [win, off], [out])
+        elif scale is None:
+            run(e, lambda: g.vector.tensor_copy(ap(out), ap(win).indirect(ap(off))), [win, off], [out])
+        else:
+            run(e, lambda: g.vector.tensor_scalar(ap(out), ap(win).indirect(ap(off)), scale, None, Op.mult), [win, off], [out])
+
+    def compose(e, out, win, off, k0):
+        if e == "va":
+            gather("a", A(out, H, C), A(win, 0, C), A(off, k0 + KV, k0 + K))
+            gather("v", A(out, 0, H), A(win, 0, C), A(off, k0, k0 + KV))
+        else:
+            gather(e, A(out, 0, C), A(win, 0, C), A(off, k0, k0 + K))
+
+    def ts(out, in0, s1, s2, op0, op1=None):
+        cols = [s for s in (s1, s2) if isinstance(s, tuple)]
+        v1, v2 = [ap(s) if isinstance(s, tuple) else s for s in (s1, s2)]
+        if op1 is None:
+            run("v", lambda: g.vector.tensor_scalar(ap(out), ap(in0), v1, None, op0), [in0] + cols, [out])
+        else:
+            run("v", lambda: g.vector.tensor_scalar(ap(out), ap(in0), v1, v2, op0, op1), [in0] + cols, [out])
+
+    def tt(out, in0, in1, op, off=None):
+        if off is None:
+            run("v", lambda: g.vector.tensor_tensor(ap(out), ap(in0), ap(in1), op), [in0, in1], [out])
+        else:
+            run("v", lambda: g.vector.tensor_tensor(ap(out), ap(in0).indirect(ap(off)), ap(in1), op), [in0, in1, off], [out])
+
+    def turn(out, in_):
+        run("v", lambda: g.vector.transpose(ap(out), ap(in_)), [in_], [out])
+
+    def scan(out, pattern, row):
+        o, p, d = A(out, 0, C), A(pattern, 0, C), A(row, 0, C)
+        run("v", lambda: g.vector.tensor_tensor_scan(ap(o), ap(p), ap(d), 0.0, Op.add, Op.max), [p, d], [o])
+
+    def ends(name, p0=0, p1=128, c1=C):
+        return A(name, 15, c1, 16, p0, p1)
+
+    def quant(q, s, x, c0, c1):
+        a, b, c = A(q, c0, c1), A(s, c0, c1), A(x, 4 * c0, 4 * c1)
+        run("v", lambda: g.vector.quantize_mx(ap(a), ap(b), ap(c)), [c], [a, b])
+
+    def pick(q2, s2, q, s, n, off):
+        o, i = A(q2, 0, n), A(q, 0, n)
+        o2, i2 = A(s2, 0, n), A(s, 0, n)
+        run("a", lambda: g.scalar.activation(ap(o2), ap(i2).indirect(ap(off)), Copy), [i2, off], [o2])
+        run("v", lambda: g.vector.tensor_copy(ap(o).bitcast(dt.uint32), ap(i).bitcast(dt.uint32).indirect(ap(off))), [i, off], [o])
+
+    def bank(k, n=C):
+        return A("ps", 512 * k, 512 * k + n)
+
+    def mm(k, wq, ws, w0, xq, xs, c0, c1):
+        o, a, b, c, d = bank(k, c1 - c0), A(wq, w0, w0 + 128), A(ws, w0, w0 + 128), A(xq, c0, c1), A(xs, c0, c1)
+        run("t", lambda: g.tensor.matmul_mx(ap(o), ap(a), ap(b), ap(c), ap(d), True, True), [a, b, c, d], [o])
+
+    def load(e, sem, d, src, codes=False):
+        run(e, lambda: queue[e].dma_start(b8(d) if codes else ap(d), src), [], [d], sem)
+
+    def store(e, sem, dst, d, codes=False):
+        run(e, lambda: queue[e].dma_start(dst, b8(d) if codes else ap(d)), [d], [], sem)
+
+    def fill(d, v):
+        run("v", lambda: g.vector.memset(ap(d), v), [], [d])
+
+    def iota(d, pattern, cm, small=True):
+        if small:
+            run("g", lambda: g.iota(ap(d), pattern, 0, cm, allow_small_or_imprecise_dtypes=True), [], [d])
+        else:
+            run("g", lambda: g.iota(ap(d), pattern, 0, cm), [], [d])
+
+    nxt, prv = T.cores[(r + 1) % N], T.cores[(r - 1) % N]
+
+    for t in range(R):
+        n = len(topo.engines(prv, core))
+        lands(A("qz%d" % t, 0, C), "z%d" % t, 2 * n)
+        lands(A("sz%d" % t, 0, C), "z%d" % t, 2 * n)
+        for q in range(N - 1):
+            if q != r:
+                for to, n in list_takers(q, len(topo.engines(T.cores[q], core))):
+                    if to == r:
+                        lands(A("ll%d" % t, K * q, K * q + K), "l%d_%d" % (t, q), n)
+
+    load("a", "dpr", A("pri", 0, K), T.pr[:])
+    load("s", "du", A("ut", 0, 512), T.u[:])
+    load("s", "dx0", A("x0", 0, 4 * H), T.x[:, 0:4 * H])
+    load("s", "dx1", A("x0", 4 * H, 4 * C), T.x[:, 4 * H:4 * C])
+    load("s", "dvc", A("vq", 0, 512), T.vc[:], True)
+    load("s", "dvs", A("vp", 0, 512), T.vs[:])
+    load("s", "dwc", A("wq", 0, 512), T.wc[:], True)
+    load("s", "dws", A("wp", 0, 512), T.ws[:])
+    load("s", "da", A("at", 0, 512), T.a[:])
+
+    iota(A("ipi", 0, 1), [[0, 1]], 1, False)
+    iota(A("jb", 0, 32), [[16, 32]], 0)
+    iota(A("jm", 0, C), [[0, K], [1, 16]], 0)
+    iota(A("idr", 0, C), [[1, C]], 0)
+    fill(A("cw", K, 32), 0.0)
+    fill(A("sc2", C, 512), 0.0)
+    ip, e1, e2 = A("ipf", 0, 1), A("e1", 0, 1), A("e2", 0, 1)
+    ts(A("ipm", 0, 1), A("ipi", 0, 1), 15, None, Op.bitwise_and)
+    copy("v", A("uoff", 0, 8), A("jb", 0, 8))
+    copy("v", ip, A("ipm", 0, 1))
+    ts(A("jw", 0, 32), A("jb", 0, 32), ip, None, Op.add)
+    ts(e1, ip, -STEP, 15 * STEP, Op.mult, Op.add)
+    ts(e2, ip, -STEP * WIDE, 15 * STEP * WIDE, Op.mult, Op.add)
+    for k in range(4):
+        ts(A("e4", k, k + 1), ip, 4 * STEP * WIDE, k - 60 * STEP * WIDE, Op.mult, Op.add)
+    turn(A("uu", 0, 32), A("jw", 0, 32))
+    turn(A("uu", 32, 64), A("jw", 0, 32))
+    copy("v", A("o4", 0, K, 1, 0, 64), A("jw", 0, K, 1, 0, 64))
+    ts(A("a0", 0, C), A("jm", 0, C), ip, 32 * STEP, Op.not_equal, Op.mult)
+    ts(A("a1", 0, C), A("a0", 0, C), -31 * STEP, None, Op.add)
+    copy("a", A("a2", 0, C), A("a1", 0, C), WIDE)
+    copy("v", A("prf", 0, K), A("pri", 0, K))
+    copy("v", A("pr16", 0, K), A("pri", 0, K))
+    tt(A("dd", 0, K), A("prf", 0, K), A("jw", 0, K), Op.subtract)
+    ts(A("tm", 0, K), A("dd", 0, K), e1, None, Op.mult)
+    tt(A("jp", 0, K), A("jw", 0, K), A("tm", 0, K), Op.subtract)
+    quant("qu", "su", "ut", 0, 128)
+    pick("qu2", "su2", "qu", "su", 128, A("uoff", 0, 8))
+
+    halves = ((0, H), (H, C))
+
+    def state(t, h):
+        c0, c1 = halves[h]
+        qx, sx = "qx%d" % t, "sx%d" % t
+        quant(qx, sx, "x%d" % t, c0, c1)
+        mm(h, "qu2" if t < R else "qa", "su2" if t < R else "sa", 0, qx, sx, c0, c1)
+        if t == R:
+            store("s", "doc%d" % h, T.oc[:, 4 * c0:4 * c1], A(qx, c0, c1), True)
+
+    def scores(t, h):
+        c0, c1 = halves[h]
+        if t < R:
+            copy("av"[h], A("sp", c0, c1), bank(h, c1 - c0))
+            copy("av"[h], A("sn", c0, c1), bank(h, c1 - c0), -1.0)
+        else:
+            copy("av"[h], A("ysb", c0, c1), bank(h, c1 - c0))
+            store("as"[h], "dy%d" % h, T.y[:, c0:c1], A("ysb", c0, c1))
+
+    def plane(name, b):
+        return A(name, C * b, C * b + C)
+
+    def emit(m):
+        order("s", [A(m, 0, C)], [])
+        g.sync.dma_start(T.ol[:], T[m][0:128:16, 0:C]).then_inc(T.sem.dol, 16)
+        count["dol"] += 16
+
+    state(0, 0)
+    state(0, 1)
+    for t in range(R):
+        x, xn, yt = "x%d" % t, "x%d" % (t + 1), "yt%d" % t
+        qy, sy, qz, sz, qp, sq = ["%s%d" % (n, t) for n in ("qy", "sy", "qz", "sz", "qp", "sq")]
+        ls, ll = "ls%d" % t, "ll%d" % t
+        last = t == R - 1
+
+        scores(t, 0)
+        scores(t, 1)
+        tt(A("vm", 0, C), A("sp", 0, C), A("sn", 0, C), Op.is_gt, A("pr16", 0, K))
+        scan("sv", "a1", "vm")
+        tt(A("tm", 0, K), ends("sv"), A("dd", 0, K), Op.mult)
+        tt(A("cw", 0, K), A("tm", 0, K), A("jp", 0, K), Op.add)
+        copy("v", A("c16", 0, K), A("cw", 0, K))
+
+        compose("a", "r0", "idr", "c16", 0)
+        turn(A("uu", 64, 96), A("cw", 0, 32))
+        for a in range(3):
+            turn(A("uu", 32, 64, 1, 32 * a + 32, 32 * a + 64), A("cw", 0, 32, 1, 32 * a, 32 * a + 32))
+        turn(A("uu", 0, 32, 1, 64, 128), A("cw", 0, 32, 1, 0, 64))
+        turn(A("wt", 0, 64), A("uu", 16, 80))
+        turn(A("wt", 64, 96), A("uu", 32, 64))
+        copy("v", A("ot", 0, 96), A("wt", 0, 96))
+        compose("va", "r1", "r0", "ot", 32)
+        compose("va", "r2", "r1", "ot", 64)
+        compose("va", "r3", "r2", "ot", 0)
+        scan("sc1", "a2", "r3")
+        ts(A("o4", 0, K, 1, 64, 128), ends("sc1", 0, 64), A("e2", 0, 1, 1, 0, 64), None, Op.subtract)
+        compose("va", "r4", "r3", "o4", 0)
+        scan("sc2", "a2", "r4")
+
+        def places(k):
+            ts(A("oy", K * k, K * k + K), ends("sc2"), 4.0, A("e4", k, k + 1), Op.mult, Op.add)
+
+        def parts(e, k, k0, k1):
+            gather(e, A(yt, 64 * k0 + k, 64 * k1, 4), A(x, 0, 4 * C), A("oy", K * k + k0, K * k + k1))
+
+        places(0)
+        parts("a", 0, 0, K)
+        if r < N - 1:
+            turn(A("bf", 0, 32, 1, 96, 128), ends("sc2", 96, 128, 512))
+            places(1)
+            copy("v", A("bf", 32, 48, 1, 96, 128), A("bf", 16, 32, 1, 96, 128))
+            places(2)
+            turn(A("bw", 0, 32, 1, 96, 128), A("bf", 16, 48, 1, 96, 128))
+            places(3)
+            for a in range(4):
+                ts(A(ls, 0, K, 1, 32 * a, 32 * a + 32), A("bw", 0, K, 1, 96, 128), A("e2", 0, 1, 1, 96, 128), None, Op.subtract)
+            order("g", [A(ls, 0, K)], [])
+            moves, at = [], 0
+            free = topo.engines(core, nxt)
+            for to, n in list_takers(r, len(free)):
+                rid, pid, _ = topo.addr(T.cores[to])
+                mask = sum(1 << k for k in free[at:at + n])
+                at += n
+                moves.append(RemoteDMATransfer(dst_ids=[DstId(rid=rid, pnc=pid)], dma_engine_mask=mask,
+                                               remote_sem=T.sem["l%d_%d" % (t, r)], src=T[ls][:],
+                                               dst=T[ll][:, K * r:K * r + K]))
+            g.remote_dma_fused(moves, local_sem=T.sem.sent)
+            count["sent"] += at
+            parts("a", 1, 0, K)
+            parts("a", 2, 0, KV)
+            parts("v", 3, 0, K)
+            parts("v", 2, KV, K)
+        else:
+            for k in (2, 1, 3):
+                places(k)
+            parts("v", 2, 0, K)
+            parts("a", 1, 0, K)
+            parts("v", 3, 0, K)
+        quant(qy, sy, yt, 0, C)
+        order("g", [A(qy, 0, C), A(sy, 0, C)], [])
+        rid, pid, _ = topo.addr(nxt)
+        mask = topo.mask(core, nxt)
+        g.remote_dma(b8(A(qz, 0, C)), b8(A(qy, 0, C)), T.sem["z%d" % t], T.sem.sent, pid, rid, mask)
+        g.remote_dma(T[sz][:], T[sy][:], T.sem["z%d" % t], T.sem.sent, pid, rid, mask)
+        count["sent"] += 2 * len(topo.engines(core, nxt))
+        if t == 0:
+            quant("qa", "sa", "at", 0, 128)
+
+        lists = [(ll, K * q) for q in range(N - 2, 0, -1)] + [(ls, 0)] if r == 0 else [(ll, K * q) for q in range(r - 2, -1, -1)]
+        done = [0]
+
+        def step(e):
+            i = done[0]
+            compose(e, "b%d" % (i % 2), "b%d" % (1 - i % 2) if i else "idr", lists[i][0], lists[i][1])
+            done[0] += 1
+
+        def wrap():
+            scan("sc3", "a2", "b%d" % (1 - done[0] % 2))
+            ts(A("ob", 0, K), ends("sc3"), e2, None, Op.subtract)
+
+        if r == 0:
+            if last:
+                emit("r4")
+            for b in range(4):
+                mm(b, "vq", "vp", 128 * b, qy, sy, 0, C)
+            for b in range(EARLY[t]):
+                copy("av"[b % 2], plane("pv", b), bank(b), 0.03125)
+            for b in range(4):
+                mm(4 + b, "wq", "wp", 128 * b, qz, sz, 0, C)
+            for _ in lists:
+                step("va")
+            for b in range(4):
+                if b >= EARLY[t]:
+                    copy("a", plane("pv", b), bank(b), 0.03125)
+                copy("a", plane("pw", b), bank(4 + b), 0.03125)
+            wrap()
+
+            def place(e, b, k0, k1):
+                tt(A(xn, 64 * k0 + b, 64 * k1, 4), plane("pw", b), A("pv", C * b + 16 * k0, C * b + 16 * k1), Op.max, A("ob", k0, k1))
+
+            first = [("v", 0, 0, K), ("v", 1, 0, K), ("v", 2, 0, KV), ("v", 3, 0, KV)]
+            second = [("v", 2, KV, K), ("v", 3, KV, K)]
+        else:
+            pick(qp, sq, qy, sy, C, A(ll, K * (r - 1), K * r))
+            for b in range(4):
+                mm(b, "vq", "vp", 128 * b, qp, sq, 0, C)
+            if last:
+                compose("a", "m1", "r4", ll, K * (r - 1))
+            beta = (ll, 0) if r == 2 else ("ob", 0)
+            plan = PLAN.get(r, "V M").split()
+            for w in plan:
+                if w == "V":
+                    for b in range(4):
+                        copy("a", plane("pv", b), bank(b))
+                elif w == "M":
+                    for b in range(4):
+                        mm(4 + b, "wq", "wp", 128 * b, qz, sz, 0, C)
+                    for b in range(4):
+                        tt(plane("pw", b), bank(4 + b), plane("pv", b), Op.max)
+                elif w == "w":
+                    wrap()
+                else:
+                    step(w)
+
+            def place(e, b, k0, k1):
+                out = A(xn, 64 * k0 + b, 64 * k1, 4)
+                if r == 1:
+                    copy(e, out, A("pw", C * b + 16 * k0, C * b + 16 * k1), 0.03125)
+                else:
+                    gather(e, out, plane("pw", b), A(beta[0], beta[1] + k0, beta[1] + k1), 0.03125)
+
+            if plan[-1] == "w":
+                first = [("a", 0, 0, KV), ("v", 2, 0, KV), ("a", 1, 0, KV), ("v", 3, 0, KV)]
+                second = [("a", 0, KV, K), ("v", 2, KV, K), ("a", 1, KV, K), ("v", 3, KV, K)]
+            else:
+                first = [("a", 0, 0, K), ("a", 1, 0, K), ("a", 2, 0, KV), ("v", 3, 0, KV)]
+                second = [("a", 2, KV, K), ("v", 3, KV, K)]
+        for w in first:
+            place(*w)
+        for w in second:
+            if w[0] == "a":
+                place(*w)
+        state(t + 1, 0)
+        for w in second:
+            if w[0] == "v":
+                place(*w)
+        state(t + 1, 1)
+
+    scores(R, 0)
+    for k in range(4):
+        store("s", "dos%d" % k, T.osc[4 * k:4 * k + 4, 0:C], A("sx%d" % R, 0, C, 1, 32 * k, 32 * k + 4))
+    scores(R, 1)
+    if r > 1:
+        compose("a", "m2", "m1", beta[0], beta[1])
+    if r > 0:
+        emit("m2" if r > 1 else "m1")
+    for s in SEMAPHORES:
+        if count[s] > waited[s]:
+            g.wait_ge(T.sem[s], count[s])

@@ -5,73 +5,37 @@ C, R, N = 416, 2, 8
 K = C // 16
 KV = 14
 H = 16 * KV
+KS = 18
+S = 16 * KS
 STEP = 2.0
-WIDE = 512.0
+MID = C // 2
+BIG = 2.0 ** 40
 FX, U8 = "float8_e4m3fn_x4", "uint8"
 
-SCRATCH = {
-    "ut": ("sbuf", [128, 512], "bfloat16"), "at": ("sbuf", [128, 512], "bfloat16"),
-    "qu": ("sbuf", [128, 128], FX), "su": ("sbuf", [128, 128], U8),
-    "qu2": ("sbuf", [128, 128], FX), "su2": ("sbuf", [128, 128], U8),
-    "qa": ("sbuf", [128, 128], FX), "sa": ("sbuf", [128, 128], U8),
-    "vq": ("sbuf", [128, 512], FX), "vp": ("sbuf", [128, 512], U8),
-    "wq": ("sbuf", [128, 512], FX), "wp": ("sbuf", [128, 512], U8),
-    "pri": ("sbuf", [128, K], "int32"), "prf": ("sbuf", [128, K], "float32"), "pr16": ("sbuf", [128, K], "uint16"),
-    "ipi": ("sbuf", [128, 1], "int32"), "ipm": ("sbuf", [128, 1], "int32"), "ipf": ("sbuf", [128, 1], "float32"),
-    "e1": ("sbuf", [128, 1], "float32"), "e2": ("sbuf", [128, 1], "float32"), "e4": ("sbuf", [128, 4], "float32"),
-    "jb": ("sbuf", [128, 32], "float32"), "jw": ("sbuf", [128, 32], "float32"), "uoff": ("sbuf", [128, 8], "uint16"),
-    "dd": ("sbuf", [128, K], "float32"), "jp": ("sbuf", [128, K], "float32"), "tm": ("sbuf", [128, K], "float32"),
-    "jm": ("sbuf", [128, C], "bfloat16"), "a0": ("sbuf", [128, C], "bfloat16"),
-    "a1": ("sbuf", [128, C], "bfloat16"), "a2": ("sbuf", [128, C], "bfloat16"),
-    "idr": ("sbuf", [128, C], "float32"),
-    "sp": ("sbuf", [128, C], "float32"), "sn": ("sbuf", [128, C], "float32"),
-    "vm": ("sbuf", [128, C], "bfloat16"), "sv": ("sbuf", [128, C], "bfloat16"),
-    "cw": ("sbuf", [128, 32], "float32"), "c16": ("sbuf", [128, K], "uint16"),
-    "uu": ("sbuf", [128, 96], "float32"), "wt": ("sbuf", [128, 96], "float32"), "ot": ("sbuf", [128, 96], "uint16"),
-    "r0": ("sbuf", [128, C], "float32"), "r1": ("sbuf", [128, C], "float32"), "r2": ("sbuf", [128, C], "float32"),
-    "r3": ("sbuf", [128, C], "float32"), "r4": ("sbuf", [128, C], "float32"),
-    "sc1": ("sbuf", [128, C], "float32"), "sc2": ("sbuf", [128, 512], "float32"), "sc3": ("sbuf", [128, C], "float32"),
-    "o4": ("sbuf", [128, K], "uint16"), "oy": ("sbuf", [128, 4 * K], "uint16"),
-    "bf": ("sbuf", [128, 48], "float32"), "bw": ("sbuf", [128, 32], "float32"),
-    "b0": ("sbuf", [128, C], "float32"), "b1": ("sbuf", [128, C], "float32"), "ob": ("sbuf", [128, K], "uint16"),
-    "m1": ("sbuf", [128, C], "float32"), "m2": ("sbuf", [128, C], "float32"),
-    "pv": ("sbuf", [128, 4 * C], "float32"), "pw": ("sbuf", [128, 4 * C], "float32"),
-    "ysb": ("sbuf", [128, C], "float32"),
-    "ps": ("psum", [128, 4096], "float32"),
-}
-for _t in range(R + 1):
-    SCRATCH["x%d" % _t] = ("sbuf", [128, 4 * C], "bfloat16")
-    SCRATCH["qx%d" % _t] = ("sbuf", [128, C], FX)
-    SCRATCH["sx%d" % _t] = ("sbuf", [128, C], U8)
-for _t in range(R):
-    SCRATCH["yt%d" % _t] = ("sbuf", [128, 4 * C], "bfloat16")
-    for _n in ("qy", "qz", "qp"):
-        SCRATCH["%s%d" % (_n, _t)] = ("sbuf", [128, C], FX)
-    for _n in ("sy", "sz", "sq"):
-        SCRATCH["%s%d" % (_n, _t)] = ("sbuf", [128, C], U8)
-    SCRATCH["ls%d" % _t] = ("sbuf", [128, K], "uint16")
-    SCRATCH["ll%d" % _t] = ("sbuf", [128, (N - 1) * K], "uint16")
+SCRATCH = {"ps": ("psum", [128, 4096], "float32"), "pri": ("sbuf", [128, K], "int32"),
+           "ipi": ("sbuf", [128, 1], "int32"), "ipm": ("sbuf", [128, 1], "int32")}
+for _d, _w, _names in (
+        ("bfloat16", 512, "ut at sc2"), ("bfloat16", C, "jm a0 a1 a2 a3 a4 idr vm sv r0 r1 r2 r3 r4 sc1 sc3 b0 b1"),
+        ("bfloat16", 48, "bf"), ("bfloat16", 32, "bw"), ("bfloat16", 4 * C, "x0 x1 x2 yt0 yt1"),
+        (FX, 128, "qu qu2 qa"), (U8, 128, "su su2 sa"), (FX, 512, "vq wq"), (U8, 512, "vp wp"),
+        (FX, C, "qx0 qx1 qx2 qy0 qy1 qz0 qz1 qp0 qp1"), (U8, C, "sx0 sx1 sx2 sy0 sy1 sz0 sz1 sq0 sq1"),
+        ("float32", 1, "ipf ip1 mid e1 e2 e3 e4"), ("float32", K, "prf dd jp tm"), ("float32", 32, "jb jw cw"),
+        ("float32", 96, "uu wt"), ("float32", C, "sp sn m1 m2 ysb"), ("float32", 4 * C, "pv pw"),
+        ("uint16", K, "pr16 c16 o4 ob ls0 ls1"), ("uint16", 8, "uoff"), ("uint16", 96, "ot"), ("uint16", 4 * K, "oy"),
+        ("uint16", (N - 1) * K, "ll0 ll1")):
+    for _n in _names.split():
+        SCRATCH[_n] = ("sbuf", [128, _w], _d)
 
 DMAS = ["dx0", "dx1", "du", "dpr", "dvc", "dvs", "dwc", "dws", "da", "doc0", "doc1", "dos0", "dos1", "dos2", "dos3",
         "dy0", "dy1", "dol"]
 PLAN = {2: "V M", 3: "va va V w M", 4: "va va V v w M", 5: "va va V v v w M", 6: "va va V v v M a w", 7: "va va V v v M a a w"}
-EARLY = [4, 2]
+ZERO = ["Va Vv Va Vv va va va va va va va Wa Wa Wa Wa w", "va va va va va Va Va v v Wa Va Wa Va Wa Wa w"]
 SEMAPHORES = (["cv", "ca", "ct", "cg", "sent"] + DMAS + ["z%d" % t for t in range(R)]
               + ["l%d_%d" % (t, q) for t in range(R) for q in range(N - 1)])
 
 
-def list_takers(q, engines):
-    to = [q + 1] + ([0] if q else []) + list(range(N - 1, q + 1, -1))
-    n = [1] * len(to)
-    grown = True
-    while grown:
-        grown = False
-        least = min(n)
-        for i in range(len(to)):
-            if n[i] == least and sum(n) + n[i] <= engines:
-                n[i] *= 2
-                grown = True
-    return list(zip(to, n))
+def list_takers(q):
+    return [q + 1] + ([0] if q else []) + list(range(N - 1, q + 1, -1))
 
 
 def rank_program(g, core, T, topo):
@@ -80,6 +44,7 @@ def rank_program(g, core, T, topo):
         return
     Op = AluOpType
     Copy = ActivationFunctionType.Copy
+    Ident = ActivationFunctionType.Identity
     queue = {"v": g.vector, "a": g.scalar, "t": g.tensor, "g": g, "s": g.sync}
     own = {"v": "cv", "a": "ca", "t": "ct", "g": "cg"}
     count = {s: 0 for s in SEMAPHORES}
@@ -189,12 +154,18 @@ def rank_program(g, core, T, topo):
     def turn(out, in_):
         run("v", lambda: g.vector.transpose(ap(out), ap(in_)), [in_], [out])
 
-    def scan(out, pattern, row):
+    def scan(out, pattern, row, op0, op1):
         o, p, d = A(out, 0, C), A(pattern, 0, C), A(row, 0, C)
-        run("v", lambda: g.vector.tensor_tensor_scan(ap(o), ap(p), ap(d), 0.0, Op.add, Op.max), [p, d], [o])
+        run("v", lambda: g.vector.tensor_tensor_scan(ap(o), ap(p), ap(d), 0.0, op0, op1), [p, d], [o])
+
+    def keep(out, row):
+        scan(out, "a2", row, Op.mult, Op.add)
 
     def ends(name, p0=0, p1=128, c1=C):
         return A(name, 15, c1, 16, p0, p1)
+
+    def number(out, in_):
+        ts(out, in_, A("e2", 0, 1, 1, in_[4], in_[5]), float(MID), Op.mult, Op.add)
 
     def quant(q, s, x, c0, c1):
         a, b, c = A(q, c0, c1), A(s, c0, c1), A(x, 4 * c0, 4 * c1)
@@ -222,11 +193,11 @@ def rank_program(g, core, T, topo):
     def fill(d, v):
         run("v", lambda: g.vector.memset(ap(d), v), [], [d])
 
-    def iota(d, pattern, cm, small=True):
+    def iota(d, pattern, cm, small=True, base=0):
         if small:
-            run("g", lambda: g.iota(ap(d), pattern, 0, cm, allow_small_or_imprecise_dtypes=True), [], [d])
+            run("g", lambda: g.iota(ap(d), pattern, base, cm, allow_small_or_imprecise_dtypes=True), [], [d])
         else:
-            run("g", lambda: g.iota(ap(d), pattern, 0, cm), [], [d])
+            run("g", lambda: g.iota(ap(d), pattern, base, cm), [], [d])
 
     nxt, prv = T.cores[(r + 1) % N], T.cores[(r - 1) % N]
 
@@ -235,15 +206,13 @@ def rank_program(g, core, T, topo):
         lands(A("qz%d" % t, 0, C), "z%d" % t, 2 * n)
         lands(A("sz%d" % t, 0, C), "z%d" % t, 2 * n)
         for q in range(N - 1):
-            if q != r:
-                for to, n in list_takers(q, len(topo.engines(T.cores[q], core))):
-                    if to == r:
-                        lands(A("ll%d" % t, K * q, K * q + K), "l%d_%d" % (t, q), n)
+            if r in list_takers(q):
+                lands(A("ll%d" % t, K * q, K * q + K), "l%d_%d" % (t, q), len(topo.engines(T.cores[q], core)))
 
     load("a", "dpr", A("pri", 0, K), T.pr[:])
     load("s", "du", A("ut", 0, 512), T.u[:])
-    load("s", "dx0", A("x0", 0, 4 * H), T.x[:, 0:4 * H])
-    load("s", "dx1", A("x0", 4 * H, 4 * C), T.x[:, 4 * H:4 * C])
+    load("s", "dx0", A("x0", 0, 4 * S), T.x[:, 0:4 * S])
+    load("s", "dx1", A("x0", 4 * S, 4 * C), T.x[:, 4 * S:4 * C])
     load("s", "dvc", A("vq", 0, 512), T.vc[:], True)
     load("s", "dvs", A("vp", 0, 512), T.vs[:])
     load("s", "dwc", A("wq", 0, 512), T.wc[:], True)
@@ -253,33 +222,37 @@ def rank_program(g, core, T, topo):
     iota(A("ipi", 0, 1), [[0, 1]], 1, False)
     iota(A("jb", 0, 32), [[16, 32]], 0)
     iota(A("jm", 0, C), [[0, K], [1, 16]], 0)
-    iota(A("idr", 0, C), [[1, C]], 0)
+    iota(A("idr", 0, C), [[1, C]], 0, True, -MID)
     fill(A("cw", K, 32), 0.0)
     fill(A("sc2", C, 512), 0.0)
-    ip, e1, e2 = A("ipf", 0, 1), A("e1", 0, 1), A("e2", 0, 1)
+    fill(A("mid", 0, 1), float(MID))
+    ip, ip1, e1, e2, e3, e4 = [A(n, 0, 1) for n in ("ipf", "ip1", "e1", "e2", "e3", "e4")]
     ts(A("ipm", 0, 1), A("ipi", 0, 1), 15, None, Op.bitwise_and)
     copy("v", A("uoff", 0, 8), A("jb", 0, 8))
     copy("v", ip, A("ipm", 0, 1))
     ts(A("jw", 0, 32), A("jb", 0, 32), ip, None, Op.add)
     ts(e1, ip, -STEP, 15 * STEP, Op.mult, Op.add)
-    ts(e2, ip, -STEP * WIDE, 15 * STEP * WIDE, Op.mult, Op.add)
-    for k in range(4):
-        ts(A("e4", k, k + 1), ip, 4 * STEP * WIDE, k - 60 * STEP * WIDE, Op.mult, Op.add)
+    ts(ip1, ip, 1.0, None, Op.add)
+    ts(e2, ip, 15.0, 1 / BIG, Op.is_equal, Op.max)
+    ts(e3, ip, 15.0, 4.0, Op.is_equal, Op.mult)
     turn(A("uu", 0, 32), A("jw", 0, 32))
     turn(A("uu", 32, 64), A("jw", 0, 32))
     copy("v", A("o4", 0, K, 1, 0, 64), A("jw", 0, K, 1, 0, 64))
+    ts(e4, e3, 4 / BIG, None, Op.max)
     ts(A("a0", 0, C), A("jm", 0, C), ip, 32 * STEP, Op.not_equal, Op.mult)
+    ts(A("a3", 0, C), A("jm", 0, C), ip1, BIG, Op.is_equal, Op.mult)
     ts(A("a1", 0, C), A("a0", 0, C), -31 * STEP, None, Op.add)
-    copy("a", A("a2", 0, C), A("a1", 0, C), WIDE)
+    copy("a", A("a4", 0, C), A("a0", 0, C), 1 / (32 * STEP))
     copy("v", A("prf", 0, K), A("pri", 0, K))
     copy("v", A("pr16", 0, K), A("pri", 0, K))
     tt(A("dd", 0, K), A("prf", 0, K), A("jw", 0, K), Op.subtract)
-    ts(A("tm", 0, K), A("dd", 0, K), e1, None, Op.mult)
-    tt(A("jp", 0, K), A("jw", 0, K), A("tm", 0, K), Op.subtract)
     quant("qu", "su", "ut", 0, 128)
+    ts(A("tm", 0, K), A("dd", 0, K), e1, None, Op.mult)
     pick("qu2", "su2", "qu", "su", 128, A("uoff", 0, 8))
+    tt(A("jp", 0, K), A("jw", 0, K), A("tm", 0, K), Op.subtract)
+    tt(A("a2", 0, C), A("a3", 0, C), A("a4", 0, C), Op.max)
 
-    halves = ((0, H), (H, C))
+    halves = ((0, S), (S, C))
 
     def state(t, h):
         c0, c1 = halves[h]
@@ -289,22 +262,8 @@ def rank_program(g, core, T, topo):
         if t == R:
             store("s", "doc%d" % h, T.oc[:, 4 * c0:4 * c1], A(qx, c0, c1), True)
 
-    def scores(t, h):
-        c0, c1 = halves[h]
-        if t < R:
-            copy("av"[h], A("sp", c0, c1), bank(h, c1 - c0))
-            copy("av"[h], A("sn", c0, c1), bank(h, c1 - c0), -1.0)
-        else:
-            copy("av"[h], A("ysb", c0, c1), bank(h, c1 - c0))
-            store("as"[h], "dy%d" % h, T.y[:, c0:c1], A("ysb", c0, c1))
-
     def plane(name, b):
         return A(name, C * b, C * b + C)
-
-    def emit(m):
-        order("s", [A(m, 0, C)], [])
-        g.sync.dma_start(T.ol[:], T[m][0:128:16, 0:C]).then_inc(T.sem.dol, 16)
-        count["dol"] += 16
 
     state(0, 0)
     state(0, 1)
@@ -312,12 +271,14 @@ def rank_program(g, core, T, topo):
         x, xn, yt = "x%d" % t, "x%d" % (t + 1), "yt%d" % t
         qy, sy, qz, sz, qp, sq = ["%s%d" % (n, t) for n in ("qy", "sy", "qz", "sz", "qp", "sq")]
         ls, ll = "ls%d" % t, "ll%d" % t
-        last = t == R - 1
 
-        scores(t, 0)
-        scores(t, 1)
-        tt(A("vm", 0, C), A("sp", 0, C), A("sn", 0, C), Op.is_gt, A("pr16", 0, K))
-        scan("sv", "a1", "vm")
+        copy("a", A("sp", 0, S), bank(0, S))
+        copy("a", A("sn", 0, S), bank(0, S), -1.0)
+        copy("v", A("sp", S, C), bank(1, C - S))
+        gather("a", A("sn", S, C), A("sp", 0, C), A("pr16", KS, K), -1.0)
+        tt(A("vm", 0, S), A("sp", 0, C), A("sn", 0, S), Op.is_gt, A("pr16", 0, KS))
+        tt(A("vm", S, C), bank(1, C - S), A("sn", S, C), Op.is_gt)
+        scan("sv", "a1", "vm", Op.add, Op.max)
         tt(A("tm", 0, K), ends("sv"), A("dd", 0, K), Op.mult)
         tt(A("cw", 0, K), A("tm", 0, K), A("jp", 0, K), Op.add)
         copy("v", A("c16", 0, K), A("cw", 0, K))
@@ -327,19 +288,19 @@ def rank_program(g, core, T, topo):
         for a in range(3):
             turn(A("uu", 32, 64, 1, 32 * a + 32, 32 * a + 64), A("cw", 0, 32, 1, 32 * a, 32 * a + 32))
         turn(A("uu", 0, 32, 1, 64, 128), A("cw", 0, 32, 1, 0, 64))
-        turn(A("wt", 0, 64), A("uu", 16, 80))
         turn(A("wt", 64, 96), A("uu", 32, 64))
+        turn(A("wt", 0, 64), A("uu", 16, 80))
         copy("v", A("ot", 0, 96), A("wt", 0, 96))
         compose("va", "r1", "r0", "ot", 32)
         compose("va", "r2", "r1", "ot", 64)
         compose("va", "r3", "r2", "ot", 0)
-        scan("sc1", "a2", "r3")
-        ts(A("o4", 0, K, 1, 64, 128), ends("sc1", 0, 64), A("e2", 0, 1, 1, 0, 64), None, Op.subtract)
+        keep("sc1", "r3")
+        number(A("o4", 0, K, 1, 64, 128), ends("sc1", 0, 64))
         compose("va", "r4", "r3", "o4", 0)
-        scan("sc2", "a2", "r4")
+        keep("sc2", "r4")
 
         def places(k):
-            ts(A("oy", K * k, K * k + K), ends("sc2"), 4.0, A("e4", k, k + 1), Op.mult, Op.add)
+            ts(A("oy", K * k, K * k + K), ends("sc2"), e4, float(4 * MID + k), Op.mult, Op.add)
 
         def parts(e, k, k0, k1):
             gather(e, A(yt, 64 * k0 + k, 64 * k1, 4), A(x, 0, 4 * C), A("oy", K * k + k0, K * k + k1))
@@ -354,19 +315,14 @@ def rank_program(g, core, T, topo):
             turn(A("bw", 0, 32, 1, 96, 128), A("bf", 16, 48, 1, 96, 128))
             places(3)
             for a in range(4):
-                ts(A(ls, 0, K, 1, 32 * a, 32 * a + 32), A("bw", 0, K, 1, 96, 128), A("e2", 0, 1, 1, 96, 128), None, Op.subtract)
+                number(A(ls, 0, K, 1, 32 * a, 32 * a + 32), A("bw", 0, K, 1, 96, 128))
             order("g", [A(ls, 0, K)], [])
-            moves, at = [], 0
-            free = topo.engines(core, nxt)
-            for to, n in list_takers(r, len(free)):
-                rid, pid, _ = topo.addr(T.cores[to])
-                mask = sum(1 << k for k in free[at:at + n])
-                at += n
-                moves.append(RemoteDMATransfer(dst_ids=[DstId(rid=rid, pnc=pid)], dma_engine_mask=mask,
-                                               remote_sem=T.sem["l%d_%d" % (t, r)], src=T[ls][:],
-                                               dst=T[ll][:, K * r:K * r + K]))
-            g.remote_dma_fused(moves, local_sem=T.sem.sent)
-            count["sent"] += at
+            to = [topo.addr(T.cores[q]) for q in list_takers(r)]
+            g.remote_dma_fused([RemoteDMATransfer(dst_ids=[DstId(rid=a[0], pnc=a[1]) for a in to],
+                                                  dma_engine_mask=topo.mask(core, nxt),
+                                                  remote_sem=T.sem["l%d_%d" % (t, r)], srcs=[T[ls][:]],
+                                                  dsts=[T[ll][:, K * r:K * r + K] for _ in to])], local_sem=T.sem.sent)
+            count["sent"] += len(topo.engines(core, nxt))
             parts("a", 1, 0, K)
             parts("a", 2, 0, KV)
             parts("v", 3, 0, K)
@@ -396,37 +352,35 @@ def rank_program(g, core, T, topo):
             done[0] += 1
 
         def wrap():
-            scan("sc3", "a2", "b%d" % (1 - done[0] % 2))
-            ts(A("ob", 0, K), ends("sc3"), e2, None, Op.subtract)
+            keep("sc3", "b%d" % (1 - done[0] % 2))
+            number(A("ob", 0, K), ends("sc3"))
 
         if r == 0:
-            if last:
-                emit("r4")
             for b in range(4):
                 mm(b, "vq", "vp", 128 * b, qy, sy, 0, C)
-            for b in range(EARLY[t]):
-                copy("av"[b % 2], plane("pv", b), bank(b), 0.03125)
-            for b in range(4):
-                mm(4 + b, "wq", "wp", 128 * b, qz, sz, 0, C)
-            for _ in lists:
-                step("va")
-            for b in range(4):
-                if b >= EARLY[t]:
-                    copy("a", plane("pv", b), bank(b), 0.03125)
-                copy("a", plane("pw", b), bank(4 + b), 0.03125)
-            wrap()
+            nv, nw = 0, 0
+            for w in ZERO[t].split():
+                if w[0] == "V":
+                    copy(w[1], plane("pv", nv), bank(nv), 0.03125)
+                    nv += 1
+                elif w[0] == "W":
+                    mm(4 + nw, "wq", "wp", 128 * nw, qz, sz, 0, C)
+                    copy(w[1], plane("pw", nw), bank(4 + nw), 0.03125)
+                    nw += 1
+                elif w == "w":
+                    wrap()
+                else:
+                    step(w)
 
             def place(e, b, k0, k1):
                 tt(A(xn, 64 * k0 + b, 64 * k1, 4), plane("pw", b), A("pv", C * b + 16 * k0, C * b + 16 * k1), Op.max, A("ob", k0, k1))
 
-            first = [("v", 0, 0, K), ("v", 1, 0, K), ("v", 2, 0, KV), ("v", 3, 0, KV)]
-            second = [("v", 2, KV, K), ("v", 3, KV, K)]
+            first = [("v", b, 0, KS) for b in range(4)]
+            second = [("v", b, KS, K) for b in range(4)]
         else:
             pick(qp, sq, qy, sy, C, A(ll, K * (r - 1), K * r))
             for b in range(4):
                 mm(b, "vq", "vp", 128 * b, qp, sq, 0, C)
-            if last:
-                compose("a", "m1", "r4", ll, K * (r - 1))
             beta = (ll, 0) if r == 2 else ("ob", 0)
             plan = PLAN.get(r, "V M").split()
             for w in plan:
@@ -451,11 +405,14 @@ def rank_program(g, core, T, topo):
                     gather(e, out, plane("pw", b), A(beta[0], beta[1] + k0, beta[1] + k1), 0.03125)
 
             if plan[-1] == "w":
-                first = [("a", 0, 0, KV), ("v", 2, 0, KV), ("a", 1, 0, KV), ("v", 3, 0, KV)]
-                second = [("a", 0, KV, K), ("v", 2, KV, K), ("a", 1, KV, K), ("v", 3, KV, K)]
+                first = [("a", 0, 0, KS), ("v", 2, 0, KS), ("a", 1, 0, KS), ("v", 3, 0, KS)]
+                second = [("a", 0, KS, K), ("a", 2, KS, K), ("a", 1, KS, K), ("v", 3, KS, K)]
+            elif r == 1:
+                first = [("a", 0, 0, K), ("a", 1, 0, K), ("a", 2, 0, K), ("v", 3, 0, KS)]
+                second = [("a", 3, KS, K)]
             else:
-                first = [("a", 0, 0, K), ("a", 1, 0, K), ("a", 2, 0, KV), ("v", 3, 0, KV)]
-                second = [("a", 2, KV, K), ("v", 3, KV, K)]
+                first = [("a", 0, 0, KS), ("a", 1, 0, KS), ("a", 2, 0, KS), ("v", 3, 0, KS)]
+                second = [("a", 0, KS, K), ("a", 1, KS, K), ("a", 2, KS, K), ("v", 3, KS, K)]
         for w in first:
             place(*w)
         for w in second:
@@ -467,14 +424,29 @@ def rank_program(g, core, T, topo):
                 place(*w)
         state(t + 1, 1)
 
-    scores(R, 0)
+    m, row, mid = A("m1", 0, C), A("r4", 0, C), A("mid", 0, 1)
+
+    def emit(d):
+        order("s", [d], [])
+        g.sync.dma_start(T.ol[:], T[d[0]][0:128:16, 0:C]).then_inc(T.sem.dol, 16)
+        count["dol"] += 16
+
+    if r == 0:
+        run("a", lambda: g.scalar.activation(ap(m), ap(row), Ident, bias=ap(mid)), [row, mid], [m])
+        emit(m)
+    copy("a", A("ysb", 0, S), bank(0, S))
+    store("a", "dy0", T.y[:, 0:S], A("ysb", 0, S))
+    copy("v", A("ysb", S, C), bank(1, C - S))
     for k in range(4):
-        store("s", "dos%d" % k, T.osc[4 * k:4 * k + 4, 0:C], A("sx%d" % R, 0, C, 1, 32 * k, 32 * k + 4))
-    scores(R, 1)
-    if r > 1:
-        compose("a", "m2", "m1", beta[0], beta[1])
+        store("sa"[k % 2], "dos%d" % k, T.osc[4 * k:4 * k + 4, 0:C], A("sx%d" % R, 0, C, 1, 32 * k, 32 * k + 4))
+    store("s", "dy1", T.y[:, S:C], A("ysb", S, C))
     if r > 0:
-        emit("m2" if r > 1 else "m1")
+        off = A(ll, K * (r - 1), K * r)
+        run("a", lambda: g.scalar.activation(ap(m), ap(row).indirect(ap(off)), Ident, bias=ap(mid)), [row, off, mid], [m])
+        if r > 1:
+            compose("va", "m2", "m1", beta[0], beta[1])
+            m = A("m2", 0, C)
+        emit(m)
     for s in SEMAPHORES:
         if count[s] > waited[s]:
             g.wait_ge(T.sem[s], count[s])

@@ -2,49 +2,402 @@ from concourse.bass import DstId, RemoteDMATransfer
 from concourse.mybir import dt, AluOpType, ActivationFunctionType
 
 C, R, N = 416, 2, 8
-K = C // 16
-KV = 14
-H = 16 * KV
-KS = 18
-S = 16 * KS
-STEP = 2.0
-MID = C // 2
-BIG = 2.0 ** 40
+K, KV, KS, SLOT = C // 16, 14, 18, 32
+S, MID, STEP, BIG = 16 * KS, C // 2, 2.0, 2.0 ** 40
 FX, U8 = "float8_e4m3fn_x4", "uint8"
+OPT = {"ychunks": ((0, 26),), "half": 5, "r0v": 6, "psplit": 2, "zero": 0, "zp": 0,
+       "ahead": (0, 0), "last": ((0, 18), (18, 26)), "early": (7, 7, 7, 7, 7, 7, 7)}
+ABC = "0123456789abcdefghijklmnopqrstuvwxyzABCDEFGHIJKLMNOPQRSTUVWXYZ!#$%&()*+,-./:;<=>?@[]^{|}~"
+ORDER = ['4000000ggg82eokeqeem0ugkmcg0e4knmkikkkkkecjiji4eeeee6c2eiee688a8888c8888a088806660ccc8aaca8444a57764442488655646504326828a993c20082b05a6234201210406442020212000020a6042002202000000002002664200zd2u00042554a85406210463a2e34355202843b4a590020640120100030214200b6201000', '002ggi200000go0qaaacqcige68i4j68ag8eg6eej48aaa0a048666604caa886446644644464022222aaacacaa624b2782432663284267243662272222ad55242222222434220000668442222202200000000008846046642205204310214268a00122bb107202500030973504202ca42020401', '0200020e8egcgccg800iac00ec04460ec22eda8cg46466a27454440222a8666644264242422222422aaa4aca8db8442534224324844754544b44944447446d987622223342222008866486420002000000020082624042420653522d24c38490062c432604247200411330232274018807430020', '008e042acceem688co84k6i000006k6kge2deg2a248c4296786664440888866046644242224222422a8846c6866722737422401523a4862b62eae28006112090110210542050030000004084404622004002020000002624b40842202645324021cc3684384h010cc8685302550035902034201224b215075100', '00000226ce4ee4a80ge80eoikklgeg4e0046e648gccc42898a8842440224864242242642422222422a8888aa8b24246475400120a8c43542c92a3a20a0663175200010a75520003000000040802224202020020200000088662242220db6452002j1c2332222846iecbf755a242003d3007b57200406022073541131', '2200000042e28cgamcas8e8cssrscm6k8488ilgg4266cb8aaa84666eeaaa88aa6686646442222222a68b82fa86604928644652a502403c6a5a9e22e32250124072250304007332052002000000a26420042002000200000086494420ff44000220f010400141602631242a10a88601412033100009732245f70220503130', '4iii4220o4c4gg000cca4cq80r042m2288ge024660ecacac0bcaa606604a48864644448444464446022aa6b82c6862d2467446243456476445248008450928810cca8203152530304020110022120000084642422000400002000200846924844409050300046n1708aec225420k30c0003318088030120005317750202022deda22201300', '24g0e0024mg80ac8e8oeq0qocec8ckeie8c0eehac82adc846662444cca26686464242222042224222b0642235222643488456a8656502297526e882025307020523004003532030302000040864426202002000200020040920552000862l51a8c6i26233eee2202497010c0031225d5000aa1022353250098052001']
 
 SCRATCH = {"ps": ("psum", [128, 4096], "float32"), "pri": ("sbuf", [128, K], "int32"),
            "ipi": ("sbuf", [128, 1], "int32"), "ipm": ("sbuf", [128, 1], "int32")}
 for _d, _w, _names in (
-        ("bfloat16", 512, "ut at sc2"), ("bfloat16", C, "jm a0 a1 a2 a3 a4 idr vm sv r0 r1 r2 r3 r4 sc1 sc3 b0 b1"),
-        ("bfloat16", 48, "bf"), ("bfloat16", 32, "bw"), ("bfloat16", 4 * C, "x0 x1 x2 yt0 yt1"),
+        ("bfloat16", 512, "ut at sc2"), ("bfloat16", C, "a1 a2 idr vm r0 r1 r2 r3 r4 sc1 sc3 sc4"),
+        ("bfloat16", 8 * C, "br"), ("bfloat16", 16, "f1 f3 f4 fa fb"), ("bfloat16", 3 * C, "sv"),
+        ("bfloat16", 48, "bf"), ("bfloat16", 32, "bw"), ("bfloat16", 4 * C, "x0 x1 x2 yt0 yt1 mb"),
         (FX, 128, "qu qu2 qa"), (U8, 128, "su su2 sa"), (FX, 512, "vq wq"), (U8, 512, "vp wp"),
-        (FX, C, "qx0 qx1 qx2 qy0 qy1 qz0 qz1 qp0 qp1"), (U8, C, "sx0 sx1 sx2 sy0 sy1 sz0 sz1 sq0 sq1"),
-        ("float32", 1, "ipf ip1 mid e1 e2 e3 e4"), ("float32", K, "prf dd jp tm"), ("float32", 32, "jb jw cw"),
-        ("float32", 96, "uu wt"), ("float32", C, "sp sn m1 m2 ysb"), ("float32", 4 * C, "pv pw"),
-        ("uint16", K, "pr16 c16 o4 ob ls0 ls1"), ("uint16", 8, "uoff"), ("uint16", 96, "ot"), ("uint16", 4 * K, "oy"),
-        ("uint16", (N - 1) * K, "ll0 ll1")):
+        (FX, C, "qx0 qx1 qx2 qy0 qy1 qz0 qz1 qp0 qp1 qr0 qr1"), (U8, C, "sx0 sx1 sx2 sy0 sy1 sz0 sz1 sq0 sq1 sr0 sr1"),
+        ("float32", 1, "ipf ip16 ip17 mid e1 e2 e4"), ("float32", K, "tm"), ("float32", 32, "jb jw"),
+        ("float32", 96, "uu wt tb cw"), ("float32", C, "sp sn m1 m2 ysb"), ("float32", 4 * C, "pv pw"),
+        ("uint16", K, "pr16 c16 o4 oh ob o16 id16 ls0 ls1"), ("uint16", 8, "uoff"), ("uint16", 96, "ot"),
+        ("uint16", 4 * K, "oy"), ("uint16", (N - 1) * SLOT, "ll0 ll1")):
     for _n in _names.split():
         SCRATCH[_n] = ("sbuf", [128, _w], _d)
 
-DMAS = ["dx0", "dx1", "du", "dpr", "dvc", "dvs", "dwc", "dws", "da", "doc0", "doc1", "dos0", "dos1", "dos2", "dos3",
-        "dy0", "dy1", "dol"]
-PLAN = {2: "V M", 3: "va va V w M", 4: "va va V v w M", 5: "va va V v v w M", 6: "va va V v v M a w", 7: "va va V v v M a a w"}
-ZERO = ["Va Vv Va Vv va va va va va va va Wa Wa Wa Wa w", "va va va va va Va Va v v Wa Va Wa Va Wa Wa w"]
-SEMAPHORES = (["cv", "ca", "ct", "cg", "sent"] + DMAS + ["z%d" % t for t in range(R)]
+SEMAPHORES = ("cv ca ct cg sent dx0 dx1 du dpr dvc dvs dwc dws da doc0 doc1 doc2 dos0 dos1 dos2 dos3 dy0 dy1 dy2 dol".split()
+              + ["z%d_%d" % (t, h) for t in range(R) for h in range(3)]
               + ["l%d_%d" % (t, q) for t in range(R) for q in range(N - 1)])
 
 
-def list_takers(q):
-    return [q + 1] + ([0] if q else []) + list(range(N - 1, q + 1, -1))
+def list_takers(q, t):
+    head = [q + 1] + ([0] if 0 < q < N - 1 - OPT["ahead"][t] else [])
+    return (head[::-1] if OPT["zero"] else head) + list(range(N - 1, q + 1, -1))
+
+
+def A(name, c0, c1, step=1, p0=0, p1=128):
+    return (name, c0, c1, step, p0, p1)
+
+
+def cols(d):
+    return (d[2] - d[1] + d[3] - 1) // d[3]
+
+
+def meet(a, b):
+    if a[0] == "ps":
+        return a[1] // 512 == b[1] // 512
+    if a[2] <= b[1] or b[2] <= a[1] or a[5] <= b[4] or b[5] <= a[4]:
+        return False
+    return not (a[3] == b[3] and a[3] > 1 and (a[1] - b[1]) % a[3])
+
+
+def steps(r):
+    out, now = [], [0]
+
+    def put(es, kind, args, reads, writes):
+        out.append((es, kind, args, reads, writes, now[0]))
+
+    def copy(es, o, i, scale=None):
+        put(es, "copy", (o, i, None, scale, None), [i], [o])
+
+    def gather(es, o, win, off, scale=None, add=None):
+        put(es, "copy", (o, win, off, scale, add), [win, off] + ([A("mid", 0, 1)] if add else []), [o])
+
+    def compose(o, win, off, es="va", add=None, kv=KV):
+        fixed = len(es) == 3
+        gather("a" if fixed else es, A(o[0], o[1] + 16 * kv, o[1] + C), win, A(off[0], off[1] + kv, off[1] + K), None, add)
+        if kv:
+            gather("v" if fixed else es, A(o[0], o[1], o[1] + 16 * kv), win, A(off[0], off[1], off[1] + kv), None, add)
+
+    def ts(o, i, s1, s2, op0, op1=None):
+        put("v", "ts", (o, i, s1, s2, op0, op1), [i] + [s for s in (s1, s2) if isinstance(s, tuple)], [o])
+
+    def tt(o, i0, i1, op, off=None):
+        put("v", "tt", (o, i0, i1, op, off), [i0, i1] + ([off] if off else []), [o])
+
+    def turn(o, i):
+        put("v", "turn", (o, i), [i], [o])
+
+    def scan(o, d0, d1, op0, op1):
+        put("v", "scan", (o, d0, d1, op0, op1), [d0, d1], [o])
+
+    def keep(o, d):
+        scan(A(o, 0, C), A("a2", 0, C), d, "mult", "add")
+
+    def ends(name, p0=0, p1=128, c1=C):
+        return A(name, 15, c1, 16, p0, p1)
+
+    def number(o, i):
+        ts(o, i, A("e2", 0, 1, 1, i[4], i[5]), float(MID), "mult", "add")
+
+    def quant(q, s, x, c0, c1):
+        a, b, c = A(q, c0, c1), A(s, c0, c1), A(x, 4 * c0, 4 * c1)
+        put("v", "quant", (a, b, c), [c], [a, b])
+
+    def pick(q2, s2, q, s, n, off, c0=0):
+        c1 = c0 + 16 * cols(off)
+        put("va", "copy", (A(s2, c0, c1), A(s, 0, n), off, None, None), [A(s, 0, n), off], [A(s2, c0, c1)])
+        put("v", "codes", (A(q2, c0, c1), A(q, 0, n), off), [A(q, 0, n), off], [A(q2, c0, c1)])
+
+    def bank(k, n=C):
+        return A("ps", 512 * k, 512 * k + n)
+
+    def mm(k, wq, ws, w0, xq, xs, c0, c1):
+        a = (bank(k, c1 - c0), A(wq, w0, w0 + 128), A(ws, w0, w0 + 128), A(xq, c0, c1), A(xs, c0, c1))
+        put("t", "mm", a, list(a[1:]), [a[0]])
+
+    def load(e, sem, d, name, c0=None, c1=None):
+        put(e, "load", (sem, d, name, c0, c1), [], [d, A("loads", 0, 1)] if e == "s" else [d])
+
+    def store(sem, name, where, d):
+        put("sa", "store", (sem, name, where, d), [d], [])
+
+    def fill(d, v):
+        put("v", "fill", (d, v), [], [d])
+
+    def iota(d, pattern, cm, small=True, base=0):
+        put("g", "iota", (d, pattern, base, cm, small), [], [d])
+
+    def row(name, c0=0):
+        return A(name, c0, c0 + C)
+
+    def plane(name, b, k0=0, k1=K):
+        return A(name, C * b + 16 * k0, C * b + 16 * k1)
+
+    def slot(t, q):
+        return A("ll%d" % t, SLOT * q, SLOT * q + K)
+
+    chunks = OPT["ychunks"]
+    for t in range(R):
+        for h, (k0, k1) in enumerate(chunks):
+            put("", "lands", ("z%d_%d" % (t, h), (r - 1) % N, 2), [], [A("qz%d" % t, 16 * k0, 16 * k1), A("sz%d" % t, 16 * k0, 16 * k1)])
+        for q in range(N - 1):
+            if r in list_takers(q, t):
+                put("", "lands", ("l%d_%d" % (t, q), q, 1), [], [slot(t, q)])
+
+    load("a", "dpr", A("pri", 0, K), "pr")
+    load("s", "du", A("ut", 0, 512), "u")
+    load("s", "dx0", A("x0", 0, 4 * S), "x", 0, 4 * S)
+    load("s", "dx1", A("x0", 4 * S, 4 * C), "x", 4 * S, 4 * C)
+    load("s", "dvc", A("vq", 0, 512), "vc")
+    load("s", "dvs", A("vp", 0, 512), "vs")
+    load("s", "dwc", A("wq", 0, 512), "wc")
+    load("s", "dws", A("wp", 0, 512), "ws")
+    load("s", "da", A("at", 0, 512), "a")
+
+    iota(A("ipi", 0, 1), [[0, 1]], 1, False)
+    iota(A("jb", 0, 32), [[16, 32]], 0)
+    iota(row("idr"), [[1, C]], 0, True, -MID)
+    fill(A("cw", 3 * K, 96), 0.0)
+    fill(A("tb", 0, 3 * K, 3), 0.0)
+    fill(A("sv", 13, 3 * C, 16), 0.0)
+    if r < N - 1:
+        fill(A("sc2", C, 512), 0.0)
+    fill(A("mid", 0, 1), float(MID))
+    ip, ip16, ip17, e1, e2, e4 = [A(n, 0, 1) for n in ("ipf", "ip16", "ip17", "e1", "e2", "e4")]
+    jb16, jw, dd, jp = A("jb", 0, 16), A("jw", 0, K), A("tb", 1, 3 * K, 3), A("tb", 2, 3 * K, 3)
+    ts(A("ipm", 0, 1), A("ipi", 0, 1), 15, None, "bitwise_and")
+    copy("v", A("uoff", 0, 8), A("jb", 0, 8))
+    copy("v", ip, A("ipm", 0, 1))
+    ts(A("jw", 0, 32), A("jb", 0, 32), ip, None, "add")
+    ts(A("o16", 0, K), A("jb", 0, K), 0.0, ip, "mult", "add")
+    ts(ip16, ip, 16.0, None, "mult")
+    ts(ip17, ip, 16.0, 16.0, "mult", "add")
+    ts(e1, ip, -STEP, 15 * STEP, "mult", "add")
+    ts(e2, ip, 15.0, 1 / BIG, "is_equal", "max")
+    ts(e4, e2, 4.0, None, "mult")
+    ts(A("f1", 0, 16), jb16, ip16, 32 * STEP, "not_equal", "mult")
+    ts(A("fa", 0, 16), A("f1", 0, 16), -31 * STEP, None, "add")
+    ts(A("f3", 0, 16), jb16, ip17, BIG, "is_equal", "mult")
+    ts(A("f4", 0, 16), jb16, ip16, None, "not_equal")
+    tt(A("fb", 0, 16), A("f3", 0, 16), A("f4", 0, 16), "max")
+    gather("a", row("a1"), A("fa", 0, 16), A("o16", 0, K))
+    gather("a", row("a2"), A("fb", 0, 16), A("o16", 0, K))
+    turn(A("uu", 0, 32), A("jw", 0, 32))
+    turn(A("uu", 32, 64), A("jw", 0, 32))
+    copy("v", A("o4", 0, K, 1, 0, 64), A("jw", 0, K, 1, 0, 64))
+    many = N - 1 if r == 0 else r - 1
+    halved = many >= OPT["half"]
+    if halved:
+        copy("v", A("oh", 0, K, 1, 0, 64), A("jw", 0, K, 1, 0, 64))
+        if many % 2:
+            copy("v", A("id16", 0, K), jw)
+    copy("v", A("pr16", 0, K), A("pri", 0, K))
+    tt(dd, A("pri", 0, K), jw, "subtract")
+    quant("qu", "su", "ut", 0, 128)
+    ts(A("tm", 0, K), dd, e1, None, "mult")
+    pick("qu2", "su2", "qu", "su", 128, A("uoff", 0, 8))
+    tt(jp, jw, A("tm", 0, K), "subtract")
+    quant("qa", "sa", "at", 0, 128)
+
+    def pieces(t):
+        return OPT["last"] if t == R else ((0, KS), (KS, K))
+
+    def state(t, h):
+        c0, c1 = [16 * k for k in pieces(t)[h]]
+        qx, sx = "qx%d" % t, "sx%d" % t
+        quant(qx, sx, "x%d" % t, c0, c1)
+        mm(4 + h, "qu2" if t < R else "qa", "su2" if t < R else "sa", 0, qx, sx, c0, c1)
+        if t == R:
+            store("doc%d" % h, "oc", (0, 128, 4 * c0, 4 * c1), A(qx, c0, c1))
+            copy("va", A("ysb", c0, c1), bank(4 + h, c1 - c0))
+            store("dy%d" % h, "y", (0, 128, c0, c1), A("ysb", c0, c1))
+        elif h == 0:
+            mm(6, "qu2", "su2", 0, qx, sx, c0, c1)
+
+    state(0, 0)
+    state(0, 1)
+    for t in range(R):
+        now[0] = t
+        x, xn, yt = "x%d" % t, "x%d" % (t + 1), "yt%d" % t
+        qy, sy, qz, sz, qp, sq = ["%s%d" % (n, t) for n in ("qy", "sy", "qz", "sz", "qp", "sq")]
+        ls, ll = "ls%d" % t, "ll%d" % t
+
+        copy("va", A("sp", 0, S), bank(4, S))
+        copy("va", A("sn", 0, S), bank(6, S), -1.0)
+        copy("va", A("sp", S, C), bank(5, C - S))
+        gather("a", A("sn", S, C), row("sp"), A("pr16", KS, K), -1.0)
+        tt(A("vm", 0, S), row("sp"), A("sn", 0, S), "is_gt", A("pr16", 0, KS))
+        tt(A("vm", S, C), bank(5, C - S), A("sn", S, C), "is_gt")
+        scan(A("sv", 0, 3 * C, 3), row("a1"), row("vm"), "add", "max")
+        scan(A("cw", 0, 3 * K), A("sv", 13, 3 * C, 16), A("tb", 0, 3 * K), "mult", "add")
+        copy("v", A("c16", 0, K), A("cw", 2, 3 * K, 3))
+
+        compose(row("r0"), row("idr"), A("c16", 0, K), "fix", None, OPT["r0v"])
+        turn(A("uu", 64, 96), A("cw", 2, 96, 3))
+        for a in range(3):
+            turn(A("uu", 32, 64, 1, 32 * a + 32, 32 * a + 64), A("cw", 2, 96, 3, 32 * a, 32 * a + 32))
+        turn(A("uu", 0, 32, 1, 64, 128), A("cw", 2, 96, 3, 0, 64))
+        turn(A("wt", 0, 32), A("uu", 48, 80))
+        copy("v", A("ot", 0, K), A("wt", 0, K))
+        turn(A("wt", 32, 64), A("uu", 32, 64))
+        turn(A("wt", 64, 96), A("uu", 16, 48))
+        copy("v", A("ot", 32, 96), A("wt", 32, 96))
+        compose(row("r1"), row("r0"), A("ot", 0, K), "fix")
+        compose(row("r2"), row("r1"), A("ot", 32, 58), "fix")
+        compose(row("r3"), row("r2"), A("ot", 64, 90), "fix")
+        keep("sc1", row("r3"))
+        number(A("o4", 0, K, 1, 64, 128), ends("sc1", 0, 64))
+        compose(row("r4"), row("r3"), A("o4", 0, K), "fix")
+        keep("sc2", row("r4"))
+
+        def tell(to):
+            if to:
+                put("g", "list", ("l%d_%d" % (t, r), A(ls, 0, K), slot(t, r), to), [A(ls, 0, K)], [A("sends", 0, 1)])
+
+        for k in range(4):
+            ts(A("oy", K * k, K * k + K), ends("sc2"), e4, float(4 * MID + k), "mult", "add")
+        if r < N - 1:
+            turn(A("bf", 0, 32, 1, 96, 128), ends("sc2", 96, 128, 512))
+            copy("v", A("bf", 32, 48, 1, 96, 128), A("bf", 16, 32, 1, 96, 128))
+            turn(A("bw", 0, 32, 1, 96, 128), A("bf", 16, 48, 1, 96, 128))
+            for a in range(4):
+                number(A(ls, 0, K, 1, 32 * a, 32 * a + 32), A("bw", 0, K, 1, 96, 128))
+            tell(list_takers(r, t)[:OPT["early"][r]])
+        for h, (k0, k1) in enumerate(chunks):
+            for k in range(4):
+                for a, b in ((k0, KV), (KV, k1)) if k < OPT["psplit"] and len(chunks) == 1 else ((k0, k1),):
+                    gather("va", A(yt, 64 * a + k, 64 * b, 4), A(x, 0, 4 * C), A("oy", K * k + a, K * k + b))
+            c0, c1 = 16 * k0, 16 * k1
+            quant(qy, sy, yt, c0, c1)
+            if r and h == len(chunks) - 1:
+                pick(qp, sq, qy, sy, C, slot(t, r - 1))
+            for a, b in ((qz, qy), (sz, sy)) if r < N - 1 or not OPT["ahead"][t] else ((qz, qp), (sz, sq)):
+                put("g", "send", ("z%d_%d" % (t, h), A(a, c0, c1), A(b, c0, c1)), [A(b, c0, c1)], [A("sends", 0, 1)])
+        if r < N - 1:
+            tell(list_takers(r, t)[OPT["early"][r]:])
+
+        if r == 0:
+            lists = [(ll, SLOT * q) for q in range(N - 2 - OPT["ahead"][t], 0, -1)] + [(ls, 0)]
+        else:
+            lists = [(ll, SLOT * q) for q in range(r - 2, -1, -1)]
+        if len(lists) > 1:
+            n = (len(lists) + 1) // 2 if halved else len(lists)
+            inner = [("id16", 0)] * (2 * n - len(lists)) + lists[n:]
+            for i in range(n):
+                name, k0 = lists[i]
+                if halved:
+                    copy("v", A(name, k0, k0 + K, 1, 0, 64), A(inner[i][0], inner[i][1], inner[i][1] + K, 1, 0, 64))
+                compose(row("br", C * i), row("br", C * i - C) if i else row("idr"), A(name, k0, k0 + K))
+            if halved:
+                keep("sc4", row("br", C * n - C))
+                number(A("oh", 0, K, 1, 64, 128), ends("sc4", 0, 64))
+                compose(row("br", C * n), row("br", C * n - C), A("oh", 0, K))
+                keep("sc3", row("br", C * n))
+                for p in (0, 64):
+                    number(A("ob", 0, K, 1, p, p + 64), ends("sc3", 64, 128))
+            else:
+                keep("sc3", row("br", C * n - C))
+                number(A("ob", 0, K), ends("sc3"))
+        beta = (ll, 0) if r == 2 else ("ob", 0)
+
+        def off(k0, k1):
+            return A(beta[0], beta[1] + k0, beta[1] + k1)
+
+        def wbank(b, h):
+            return b if h % 2 else 4 + b
+
+        def scaled(k0, k1):
+            km = (k0 + k1) // 2
+            for a, b in ((k0, km), (km, k1)):
+                copy("va", A(xn, 64 * a, 64 * b), A("mb", 64 * a, 64 * b), 0.03125)
+
+        if r == 0 and OPT["zp"]:
+            for b in range(4):
+                mm(b, "vq", "vp", 128 * b, qy, sy, 0, C)
+                copy("va", plane("pv", b), bank(b))
+            for h, (k0, k1) in enumerate(pieces(t + 1)):
+                pick("qr%d" % t, "sr%d" % t, qz, sz, C, off(k0, k1), 16 * k0)
+                for b in range(4):
+                    mm(wbank(b, h), "wq", "wp", 128 * b, "qr%d" % t, "sr%d" % t, 16 * k0, 16 * k1)
+                    tt(A("mb", 64 * k0 + b, 64 * k1, 4), bank(wbank(b, h), 16 * (k1 - k0)), plane("pv", b, k0, k1), "max")
+                scaled(k0, k1)
+                state(t + 1, h)
+            continue
+        if r == 0:
+            for b in range(4):
+                mm(b, "vq", "vp", 128 * b, qy, sy, 0, C)
+                copy("va", plane("pv", b), bank(b), 0.03125)
+            for h, (k0, k1) in enumerate(chunks):
+                for b in range(4):
+                    mm(wbank(b, h), "wq", "wp", 128 * b, qz, sz, 16 * k0, 16 * k1)
+                    copy("va", plane("pw", b, k0, k1), bank(wbank(b, h), 16 * (k1 - k0)), 0.03125)
+
+            def place(b, k0, k1):
+                tt(A(xn, 64 * k0 + b, 64 * k1, 4), plane("pw", b), plane("pv", b, k0, k1), "max", off(k0, k1))
+        else:
+            for b in range(4):
+                mm(b, "vq", "vp", 128 * b, qp, sq, 0, C)
+                copy("va", plane("pv", b), bank(b))
+            for h, (k0, k1) in enumerate(chunks):
+                for b in range(4):
+                    mm(wbank(b, h), "wq", "wp", 128 * b, qz, sz, 16 * k0, 16 * k1)
+                    tt(plane("pw", b, k0, k1), bank(wbank(b, h), 16 * (k1 - k0)), plane("pv", b, k0, k1), "max")
+
+            def place(b, k0, k1):
+                o = A(xn, 64 * k0 + b, 64 * k1, 4)
+                if r == 1:
+                    copy("va", o, plane("pw", b, k0, k1), 0.03125)
+                else:
+                    gather("va", o, plane("pw", b), off(k0, k1), 0.03125)
+
+        for h, (k0, k1) in enumerate(pieces(t + 1)):
+            for b in (3, 2, 1, 0):
+                place(b, k0, k1)
+            state(t + 1, h)
+
+    m = row("m1")
+    if r == 0:
+        put("va", "copy", (m, row("r4"), None, None, float(MID)), [row("r4"), A("mid", 0, 1)], [m])
+    else:
+        compose(m, row("r4"), slot(R - 1, r - 1), "va", float(MID))
+        if r > 1:
+            compose(row("m2"), m, off(0, K))
+            m = row("m2")
+    store("dol", "ol", (0, 8, 0, C), m)
+    for k in range(4):
+        store("dos%d" % k, "osc", (4 * k, 4 * k + 4, 0, C), A("sx%d" % R, 0, C, 1, 32 * k, 32 * k + 4))
+    return out
+
+
+def needs(every):
+    seen, out = {}, []
+    for i, st in enumerate(every):
+        mine = [(d, False) for d in st[3]] + [(d, True) for d in st[4]]
+        need, true = set(), set()
+        for d, w in mine:
+            for o, ow, j in seen.get(d[0], []):
+                if (w or ow or d[0] == "ps") and meet(d, o):
+                    need.add(j)
+                    if ow and not w:
+                        true.add(j)
+        for d, w in mine:
+            seen.setdefault(d[0], []).append((d, w, i))
+        out.append((need, true))
+    return out
+
+
+def ordered(every, word):
+    before = [n for n, _ in needs(every)]
+    done = set(i for i, st in enumerate(every) if st[1] == "lands")
+    out = []
+    for k in range(len(every) - len(done)):
+        ready = [i for i in range(len(every)) if i not in done and before[i] <= done]
+        x = ABC.index(word[k]) if word else 0
+        out.append((ready[x // 2], every[ready[x // 2]][0][x % 2]))
+        done.add(ready[x // 2])
+    return out
 
 
 def rank_program(g, core, T, topo):
     r = T.rank_of(core)
     if r is None:
         return
-    Op = AluOpType
-    Copy = ActivationFunctionType.Copy
-    Ident = ActivationFunctionType.Identity
+    every = steps(r)
+    Op = {"add": AluOpType.add, "subtract": AluOpType.subtract, "mult": AluOpType.mult, "max": AluOpType.max,
+          "is_gt": AluOpType.is_gt, "is_equal": AluOpType.is_equal, "not_equal": AluOpType.not_equal,
+          "bitwise_and": AluOpType.bitwise_and}
+    Copy, Ident = ActivationFunctionType.Copy, ActivationFunctionType.Identity
     queue = {"v": g.vector, "a": g.scalar, "t": g.tensor, "g": g, "s": g.sync}
     own = {"v": "cv", "a": "ca", "t": "ct", "g": "cg"}
     count = {s: 0 for s in SEMAPHORES}
@@ -52,30 +405,13 @@ def rank_program(g, core, T, topo):
     clock = {e: {} for e in queue}
     log = {}
 
-    def A(name, c0, c1, step=1, p0=0, p1=128):
-        return (name, c0, c1, step, p0, p1)
-
     def ap(d):
         if d[3] == 1:
             return T[d[0]][d[4]:d[5], d[1]:d[2]]
         return T[d[0]][d[4]:d[5], d[1]:d[2]:d[3]]
 
-    def meet(a, b):
-        if a[0] == "ps":
-            return a[1] // 512 == b[1] // 512
-        if a[2] <= b[1] or b[2] <= a[1] or a[5] <= b[4] or b[5] <= a[4]:
-            return False
-        if a[3] == b[3] and a[3] > 1 and (a[1] - b[1]) % a[3]:
-            return False
-        return True
-
-    def wait(e, sem, val, seen):
-        if clock[e].get(sem, 0) >= val:
-            return
-        queue[e].wait_ge(T.sem[sem], val)
-        waited[sem] = max(waited[sem], val)
-        for s, v in seen.items():
-            clock[e][s] = max(clock[e].get(s, 0), v)
+    def raw(d):
+        return ap(d).bitcast(dt.uint8) if SCRATCH[d[0]][2] == FX else ap(d)
 
     def order(e, reads, writes):
         need = {}
@@ -85,7 +421,11 @@ def rank_program(g, core, T, topo):
                     if sem not in need or need[sem][0] < val:
                         need[sem] = (val, seen)
         for sem, (val, seen) in sorted(need.items(), key=lambda kv: -len(kv[1][1])):
-            wait(e, sem, val, seen)
+            if clock[e].get(sem, 0) < val:
+                queue[e].wait_ge(T.sem[sem], val)
+                waited[sem] = max(waited[sem], val)
+                for s, v in seen.items():
+                    clock[e][s] = max(clock[e].get(s, 0), v)
 
     def note(e, reads, writes, sem, val):
         seen = dict(clock[e]) if e else {}
@@ -93,360 +433,74 @@ def rank_program(g, core, T, topo):
         for d, w in [(d, False) for d in reads] + [(d, True) for d in writes]:
             log.setdefault(d[0], []).append((d, w, e, sem, val, seen))
 
-    def run(e, call, reads, writes, sem=None):
-        order(e, reads, writes)
-        n = 16 if sem else 1
-        sem = sem or own[e]
-        call().then_inc(T.sem[sem], n)
-        count[sem] += n
-        note(e, reads, writes, sem, count[sem])
+    def call(e, kind, a):
+        v = g.vector
+        if kind == "copy":
+            o, i, off, scale, add = a
+            src = ap(i).indirect(ap(off)) if off else ap(i)
+            if e == "a":
+                if add:
+                    return g.scalar.activation(ap(o), src, Ident, bias=ap(A("mid", 0, 1)))
+                if scale:
+                    return g.scalar.activation(ap(o), src, Copy, scale=scale)
+                return g.scalar.activation(ap(o), src, Copy)
+            if add or scale:
+                return v.tensor_scalar(ap(o), src, add or scale, None, Op["add" if add else "mult"])
+            return v.tensor_copy(ap(o), src)
+        if kind == "codes":
+            return v.tensor_copy(ap(a[0]).bitcast(dt.uint32), ap(a[1]).bitcast(dt.uint32).indirect(ap(a[2])))
+        if kind == "ts":
+            v1, v2 = [ap(s) if isinstance(s, tuple) else s for s in a[2:4]]
+            if a[5] is None:
+                return v.tensor_scalar(ap(a[0]), ap(a[1]), v1, None, Op[a[4]])
+            return v.tensor_scalar(ap(a[0]), ap(a[1]), v1, v2, Op[a[4]], Op[a[5]])
+        if kind == "tt":
+            return v.tensor_tensor(ap(a[0]), ap(a[1]).indirect(ap(a[4])) if a[4] else ap(a[1]), ap(a[2]), Op[a[3]])
+        if kind == "turn":
+            return v.transpose(ap(a[0]), ap(a[1]))
+        if kind == "scan":
+            return v.tensor_tensor_scan(ap(a[0]), ap(a[1]), ap(a[2]), 0.0, Op[a[3]], Op[a[4]])
+        if kind == "quant":
+            return v.quantize_mx(ap(a[0]), ap(a[1]), ap(a[2]))
+        if kind == "mm":
+            return g.tensor.matmul_mx(ap(a[0]), ap(a[1]), ap(a[2]), ap(a[3]), ap(a[4]), True, True)
+        if kind == "fill":
+            return v.memset(ap(a[0]), a[1])
+        if kind == "iota":
+            if a[4]:
+                return g.iota(ap(a[0]), a[1], a[2], a[3], allow_small_or_imprecise_dtypes=True)
+            return g.iota(ap(a[0]), a[1], a[2], a[3])
+        if kind == "load":
+            return queue[e].dma_start(raw(a[1]), T[a[2]][:] if a[3] is None else T[a[2]][:, a[3]:a[4]])
+        p0, p1, c0, c1 = a[2]
+        if a[1] == "ol":
+            return queue[e].dma_start(T.ol[:], T[a[3][0]][0:128:16, 0:C])
+        return queue[e].dma_start(T[a[1]][p0:p1, c0:c1], raw(a[3]))
 
-    def lands(d, sem, n):
-        count[sem] = n
-        note(None, [], [d], sem, n)
+    nxt = T.cores[(r + 1) % N]
+    for _, kind, a, _, writes, _ in every:
+        if kind == "lands":
+            count[a[0]] = a[2] * len(topo.engines(T.cores[a[1]], core))
+            note(None, [], writes, a[0], count[a[0]])
 
-    def b8(d):
-        return ap(d).bitcast(dt.uint8)
-
-    def copy(e, out, in_, scale=None):
-        if e == "a":
-            if scale is None:
-                run(e, lambda: g.scalar.activation(ap(out), ap(in_), Copy), [in_], [out])
-            else:
-                run(e, lambda: g.scalar.activation(ap(out), ap(in_), Copy, scale=scale), [in_], [out])
-        elif scale is None:
-            run(e, lambda: g.vector.tensor_copy(ap(out), ap(in_)), [in_], [out])
-        else:
-            run(e, lambda: g.vector.tensor_scalar(ap(out), ap(in_), scale, None, Op.mult), [in_], [out])
-
-    def gather(e, out, win, off, scale=None):
-        if e == "a":
-            if scale is None:
-                run(e, lambda: g.scalar.activation(ap(out), ap(win).indirect(ap(off)), Copy), [win, off], [out])
-            else:
-                run(e, lambda: g.scalar.activation(ap(out), ap(win).indirect(ap(off)), Copy, scale=scale), [win, off], [out])
-        elif scale is None:
-            run(e, lambda: g.vector.tensor_copy(ap(out), ap(win).indirect(ap(off))), [win, off], [out])
-        else:
-            run(e, lambda: g.vector.tensor_scalar(ap(out), ap(win).indirect(ap(off)), scale, None, Op.mult), [win, off], [out])
-
-    def compose(e, out, win, off, k0):
-        if e == "va":
-            gather("a", A(out, H, C), A(win, 0, C), A(off, k0 + KV, k0 + K))
-            gather("v", A(out, 0, H), A(win, 0, C), A(off, k0, k0 + KV))
-        else:
-            gather(e, A(out, 0, C), A(win, 0, C), A(off, k0, k0 + K))
-
-    def ts(out, in0, s1, s2, op0, op1=None):
-        cols = [s for s in (s1, s2) if isinstance(s, tuple)]
-        v1, v2 = [ap(s) if isinstance(s, tuple) else s for s in (s1, s2)]
-        if op1 is None:
-            run("v", lambda: g.vector.tensor_scalar(ap(out), ap(in0), v1, None, op0), [in0] + cols, [out])
-        else:
-            run("v", lambda: g.vector.tensor_scalar(ap(out), ap(in0), v1, v2, op0, op1), [in0] + cols, [out])
-
-    def tt(out, in0, in1, op, off=None):
-        if off is None:
-            run("v", lambda: g.vector.tensor_tensor(ap(out), ap(in0), ap(in1), op), [in0, in1], [out])
-        else:
-            run("v", lambda: g.vector.tensor_tensor(ap(out), ap(in0).indirect(ap(off)), ap(in1), op), [in0, in1, off], [out])
-
-    def turn(out, in_):
-        run("v", lambda: g.vector.transpose(ap(out), ap(in_)), [in_], [out])
-
-    def scan(out, pattern, row, op0, op1):
-        o, p, d = A(out, 0, C), A(pattern, 0, C), A(row, 0, C)
-        run("v", lambda: g.vector.tensor_tensor_scan(ap(o), ap(p), ap(d), 0.0, op0, op1), [p, d], [o])
-
-    def keep(out, row):
-        scan(out, "a2", row, Op.mult, Op.add)
-
-    def ends(name, p0=0, p1=128, c1=C):
-        return A(name, 15, c1, 16, p0, p1)
-
-    def number(out, in_):
-        ts(out, in_, A("e2", 0, 1, 1, in_[4], in_[5]), float(MID), Op.mult, Op.add)
-
-    def quant(q, s, x, c0, c1):
-        a, b, c = A(q, c0, c1), A(s, c0, c1), A(x, 4 * c0, 4 * c1)
-        run("v", lambda: g.vector.quantize_mx(ap(a), ap(b), ap(c)), [c], [a, b])
-
-    def pick(q2, s2, q, s, n, off):
-        o, i = A(q2, 0, n), A(q, 0, n)
-        o2, i2 = A(s2, 0, n), A(s, 0, n)
-        run("a", lambda: g.scalar.activation(ap(o2), ap(i2).indirect(ap(off)), Copy), [i2, off], [o2])
-        run("v", lambda: g.vector.tensor_copy(ap(o).bitcast(dt.uint32), ap(i).bitcast(dt.uint32).indirect(ap(off))), [i, off], [o])
-
-    def bank(k, n=C):
-        return A("ps", 512 * k, 512 * k + n)
-
-    def mm(k, wq, ws, w0, xq, xs, c0, c1):
-        o, a, b, c, d = bank(k, c1 - c0), A(wq, w0, w0 + 128), A(ws, w0, w0 + 128), A(xq, c0, c1), A(xs, c0, c1)
-        run("t", lambda: g.tensor.matmul_mx(ap(o), ap(a), ap(b), ap(c), ap(d), True, True), [a, b, c, d], [o])
-
-    def load(e, sem, d, src, codes=False):
-        run(e, lambda: queue[e].dma_start(b8(d) if codes else ap(d), src), [], [d], sem)
-
-    def store(e, sem, dst, d, codes=False):
-        run(e, lambda: queue[e].dma_start(dst, b8(d) if codes else ap(d)), [d], [], sem)
-
-    def fill(d, v):
-        run("v", lambda: g.vector.memset(ap(d), v), [], [d])
-
-    def iota(d, pattern, cm, small=True, base=0):
-        if small:
-            run("g", lambda: g.iota(ap(d), pattern, base, cm, allow_small_or_imprecise_dtypes=True), [], [d])
-        else:
-            run("g", lambda: g.iota(ap(d), pattern, base, cm), [], [d])
-
-    nxt, prv = T.cores[(r + 1) % N], T.cores[(r - 1) % N]
-
-    for t in range(R):
-        n = len(topo.engines(prv, core))
-        lands(A("qz%d" % t, 0, C), "z%d" % t, 2 * n)
-        lands(A("sz%d" % t, 0, C), "z%d" % t, 2 * n)
-        for q in range(N - 1):
-            if r in list_takers(q):
-                lands(A("ll%d" % t, K * q, K * q + K), "l%d_%d" % (t, q), len(topo.engines(T.cores[q], core)))
-
-    load("a", "dpr", A("pri", 0, K), T.pr[:])
-    load("s", "du", A("ut", 0, 512), T.u[:])
-    load("s", "dx0", A("x0", 0, 4 * S), T.x[:, 0:4 * S])
-    load("s", "dx1", A("x0", 4 * S, 4 * C), T.x[:, 4 * S:4 * C])
-    load("s", "dvc", A("vq", 0, 512), T.vc[:], True)
-    load("s", "dvs", A("vp", 0, 512), T.vs[:])
-    load("s", "dwc", A("wq", 0, 512), T.wc[:], True)
-    load("s", "dws", A("wp", 0, 512), T.ws[:])
-    load("s", "da", A("at", 0, 512), T.a[:])
-
-    iota(A("ipi", 0, 1), [[0, 1]], 1, False)
-    iota(A("jb", 0, 32), [[16, 32]], 0)
-    iota(A("jm", 0, C), [[0, K], [1, 16]], 0)
-    iota(A("idr", 0, C), [[1, C]], 0, True, -MID)
-    fill(A("cw", K, 32), 0.0)
-    fill(A("sc2", C, 512), 0.0)
-    fill(A("mid", 0, 1), float(MID))
-    ip, ip1, e1, e2, e3, e4 = [A(n, 0, 1) for n in ("ipf", "ip1", "e1", "e2", "e3", "e4")]
-    ts(A("ipm", 0, 1), A("ipi", 0, 1), 15, None, Op.bitwise_and)
-    copy("v", A("uoff", 0, 8), A("jb", 0, 8))
-    copy("v", ip, A("ipm", 0, 1))
-    ts(A("jw", 0, 32), A("jb", 0, 32), ip, None, Op.add)
-    ts(e1, ip, -STEP, 15 * STEP, Op.mult, Op.add)
-    ts(ip1, ip, 1.0, None, Op.add)
-    ts(e2, ip, 15.0, 1 / BIG, Op.is_equal, Op.max)
-    ts(e3, ip, 15.0, 4.0, Op.is_equal, Op.mult)
-    turn(A("uu", 0, 32), A("jw", 0, 32))
-    turn(A("uu", 32, 64), A("jw", 0, 32))
-    copy("v", A("o4", 0, K, 1, 0, 64), A("jw", 0, K, 1, 0, 64))
-    ts(e4, e3, 4 / BIG, None, Op.max)
-    ts(A("a0", 0, C), A("jm", 0, C), ip, 32 * STEP, Op.not_equal, Op.mult)
-    ts(A("a3", 0, C), A("jm", 0, C), ip1, BIG, Op.is_equal, Op.mult)
-    ts(A("a1", 0, C), A("a0", 0, C), -31 * STEP, None, Op.add)
-    copy("a", A("a4", 0, C), A("a0", 0, C), 1 / (32 * STEP))
-    copy("v", A("prf", 0, K), A("pri", 0, K))
-    copy("v", A("pr16", 0, K), A("pri", 0, K))
-    tt(A("dd", 0, K), A("prf", 0, K), A("jw", 0, K), Op.subtract)
-    quant("qu", "su", "ut", 0, 128)
-    ts(A("tm", 0, K), A("dd", 0, K), e1, None, Op.mult)
-    pick("qu2", "su2", "qu", "su", 128, A("uoff", 0, 8))
-    tt(A("jp", 0, K), A("jw", 0, K), A("tm", 0, K), Op.subtract)
-    tt(A("a2", 0, C), A("a3", 0, C), A("a4", 0, C), Op.max)
-
-    halves = ((0, S), (S, C))
-
-    def state(t, h):
-        c0, c1 = halves[h]
-        qx, sx = "qx%d" % t, "sx%d" % t
-        quant(qx, sx, "x%d" % t, c0, c1)
-        mm(h, "qu2" if t < R else "qa", "su2" if t < R else "sa", 0, qx, sx, c0, c1)
-        if t == R:
-            store("s", "doc%d" % h, T.oc[:, 4 * c0:4 * c1], A(qx, c0, c1), True)
-
-    def plane(name, b):
-        return A(name, C * b, C * b + C)
-
-    state(0, 0)
-    state(0, 1)
-    for t in range(R):
-        x, xn, yt = "x%d" % t, "x%d" % (t + 1), "yt%d" % t
-        qy, sy, qz, sz, qp, sq = ["%s%d" % (n, t) for n in ("qy", "sy", "qz", "sz", "qp", "sq")]
-        ls, ll = "ls%d" % t, "ll%d" % t
-
-        copy("a", A("sp", 0, S), bank(0, S))
-        copy("a", A("sn", 0, S), bank(0, S), -1.0)
-        copy("v", A("sp", S, C), bank(1, C - S))
-        gather("a", A("sn", S, C), A("sp", 0, C), A("pr16", KS, K), -1.0)
-        tt(A("vm", 0, S), A("sp", 0, C), A("sn", 0, S), Op.is_gt, A("pr16", 0, KS))
-        tt(A("vm", S, C), bank(1, C - S), A("sn", S, C), Op.is_gt)
-        scan("sv", "a1", "vm", Op.add, Op.max)
-        tt(A("tm", 0, K), ends("sv"), A("dd", 0, K), Op.mult)
-        tt(A("cw", 0, K), A("tm", 0, K), A("jp", 0, K), Op.add)
-        copy("v", A("c16", 0, K), A("cw", 0, K))
-
-        compose("a", "r0", "idr", "c16", 0)
-        turn(A("uu", 64, 96), A("cw", 0, 32))
-        for a in range(3):
-            turn(A("uu", 32, 64, 1, 32 * a + 32, 32 * a + 64), A("cw", 0, 32, 1, 32 * a, 32 * a + 32))
-        turn(A("uu", 0, 32, 1, 64, 128), A("cw", 0, 32, 1, 0, 64))
-        turn(A("wt", 64, 96), A("uu", 32, 64))
-        turn(A("wt", 0, 64), A("uu", 16, 80))
-        copy("v", A("ot", 0, 96), A("wt", 0, 96))
-        compose("va", "r1", "r0", "ot", 32)
-        compose("va", "r2", "r1", "ot", 64)
-        compose("va", "r3", "r2", "ot", 0)
-        keep("sc1", "r3")
-        number(A("o4", 0, K, 1, 64, 128), ends("sc1", 0, 64))
-        compose("va", "r4", "r3", "o4", 0)
-        keep("sc2", "r4")
-
-        def places(k):
-            ts(A("oy", K * k, K * k + K), ends("sc2"), e4, float(4 * MID + k), Op.mult, Op.add)
-
-        def parts(e, k, k0, k1):
-            gather(e, A(yt, 64 * k0 + k, 64 * k1, 4), A(x, 0, 4 * C), A("oy", K * k + k0, K * k + k1))
-
-        places(0)
-        parts("a", 0, 0, K)
-        if r < N - 1:
-            turn(A("bf", 0, 32, 1, 96, 128), ends("sc2", 96, 128, 512))
-            places(1)
-            copy("v", A("bf", 32, 48, 1, 96, 128), A("bf", 16, 32, 1, 96, 128))
-            places(2)
-            turn(A("bw", 0, 32, 1, 96, 128), A("bf", 16, 48, 1, 96, 128))
-            places(3)
-            for a in range(4):
-                number(A(ls, 0, K, 1, 32 * a, 32 * a + 32), A("bw", 0, K, 1, 96, 128))
-            order("g", [A(ls, 0, K)], [])
-            to = [topo.addr(T.cores[q]) for q in list_takers(r)]
-            g.remote_dma_fused([RemoteDMATransfer(dst_ids=[DstId(rid=a[0], pnc=a[1]) for a in to],
-                                                  dma_engine_mask=topo.mask(core, nxt),
-                                                  remote_sem=T.sem["l%d_%d" % (t, r)], srcs=[T[ls][:]],
-                                                  dsts=[T[ll][:, K * r:K * r + K] for _ in to])], local_sem=T.sem.sent)
+    for i, e in ordered(every, ORDER[r] if ORDER else None):
+        _, kind, a, reads, writes, _ = every[i]
+        order(e, reads, [d for d in writes if d[0] in SCRATCH])
+        if kind == "list":
+            to = [topo.addr(T.cores[q]) for q in a[3]]
+            g.remote_dma_fused([RemoteDMATransfer(dst_ids=[DstId(rid=x[0], pnc=x[1]) for x in to],
+                                                  dma_engine_mask=topo.mask(core, nxt), remote_sem=T.sem[a[0]],
+                                                  srcs=[ap(a[1])], dsts=[ap(a[2]) for _ in to])], local_sem=T.sem.sent)
             count["sent"] += len(topo.engines(core, nxt))
-            parts("a", 1, 0, K)
-            parts("a", 2, 0, KV)
-            parts("v", 3, 0, K)
-            parts("v", 2, KV, K)
+        elif kind == "send":
+            rid, pid, _ = topo.addr(nxt)
+            g.remote_dma(raw(a[1]), raw(a[2]), T.sem[a[0]], T.sem.sent, pid, rid, topo.mask(core, nxt))
+            count["sent"] += len(topo.engines(core, nxt))
         else:
-            for k in (2, 1, 3):
-                places(k)
-            parts("v", 2, 0, K)
-            parts("a", 1, 0, K)
-            parts("v", 3, 0, K)
-        quant(qy, sy, yt, 0, C)
-        order("g", [A(qy, 0, C), A(sy, 0, C)], [])
-        rid, pid, _ = topo.addr(nxt)
-        mask = topo.mask(core, nxt)
-        g.remote_dma(b8(A(qz, 0, C)), b8(A(qy, 0, C)), T.sem["z%d" % t], T.sem.sent, pid, rid, mask)
-        g.remote_dma(T[sz][:], T[sy][:], T.sem["z%d" % t], T.sem.sent, pid, rid, mask)
-        count["sent"] += 2 * len(topo.engines(core, nxt))
-        if t == 0:
-            quant("qa", "sa", "at", 0, 128)
-
-        lists = [(ll, K * q) for q in range(N - 2, 0, -1)] + [(ls, 0)] if r == 0 else [(ll, K * q) for q in range(r - 2, -1, -1)]
-        done = [0]
-
-        def step(e):
-            i = done[0]
-            compose(e, "b%d" % (i % 2), "b%d" % (1 - i % 2) if i else "idr", lists[i][0], lists[i][1])
-            done[0] += 1
-
-        def wrap():
-            keep("sc3", "b%d" % (1 - done[0] % 2))
-            number(A("ob", 0, K), ends("sc3"))
-
-        if r == 0:
-            for b in range(4):
-                mm(b, "vq", "vp", 128 * b, qy, sy, 0, C)
-            nv, nw = 0, 0
-            for w in ZERO[t].split():
-                if w[0] == "V":
-                    copy(w[1], plane("pv", nv), bank(nv), 0.03125)
-                    nv += 1
-                elif w[0] == "W":
-                    mm(4 + nw, "wq", "wp", 128 * nw, qz, sz, 0, C)
-                    copy(w[1], plane("pw", nw), bank(4 + nw), 0.03125)
-                    nw += 1
-                elif w == "w":
-                    wrap()
-                else:
-                    step(w)
-
-            def place(e, b, k0, k1):
-                tt(A(xn, 64 * k0 + b, 64 * k1, 4), plane("pw", b), A("pv", C * b + 16 * k0, C * b + 16 * k1), Op.max, A("ob", k0, k1))
-
-            first = [("v", b, 0, KS) for b in range(4)]
-            second = [("v", b, KS, K) for b in range(4)]
-        else:
-            pick(qp, sq, qy, sy, C, A(ll, K * (r - 1), K * r))
-            for b in range(4):
-                mm(b, "vq", "vp", 128 * b, qp, sq, 0, C)
-            beta = (ll, 0) if r == 2 else ("ob", 0)
-            plan = PLAN.get(r, "V M").split()
-            for w in plan:
-                if w == "V":
-                    for b in range(4):
-                        copy("a", plane("pv", b), bank(b))
-                elif w == "M":
-                    for b in range(4):
-                        mm(4 + b, "wq", "wp", 128 * b, qz, sz, 0, C)
-                    for b in range(4):
-                        tt(plane("pw", b), bank(4 + b), plane("pv", b), Op.max)
-                elif w == "w":
-                    wrap()
-                else:
-                    step(w)
-
-            def place(e, b, k0, k1):
-                out = A(xn, 64 * k0 + b, 64 * k1, 4)
-                if r == 1:
-                    copy(e, out, A("pw", C * b + 16 * k0, C * b + 16 * k1), 0.03125)
-                else:
-                    gather(e, out, plane("pw", b), A(beta[0], beta[1] + k0, beta[1] + k1), 0.03125)
-
-            if plan[-1] == "w":
-                first = [("a", 0, 0, KS), ("v", 2, 0, KS), ("a", 1, 0, KS), ("v", 3, 0, KS)]
-                second = [("a", 0, KS, K), ("a", 2, KS, K), ("a", 1, KS, K), ("v", 3, KS, K)]
-            elif r == 1:
-                first = [("a", 0, 0, K), ("a", 1, 0, K), ("a", 2, 0, K), ("v", 3, 0, KS)]
-                second = [("a", 3, KS, K)]
-            else:
-                first = [("a", 0, 0, KS), ("a", 1, 0, KS), ("a", 2, 0, KS), ("v", 3, 0, KS)]
-                second = [("a", 0, KS, K), ("a", 1, KS, K), ("a", 2, KS, K), ("v", 3, KS, K)]
-        for w in first:
-            place(*w)
-        for w in second:
-            if w[0] == "a":
-                place(*w)
-        state(t + 1, 0)
-        for w in second:
-            if w[0] == "v":
-                place(*w)
-        state(t + 1, 1)
-
-    m, row, mid = A("m1", 0, C), A("r4", 0, C), A("mid", 0, 1)
-
-    def emit(d):
-        order("s", [d], [])
-        g.sync.dma_start(T.ol[:], T[d[0]][0:128:16, 0:C]).then_inc(T.sem.dol, 16)
-        count["dol"] += 16
-
-    if r == 0:
-        run("a", lambda: g.scalar.activation(ap(m), ap(row), Ident, bias=ap(mid)), [row, mid], [m])
-        emit(m)
-    copy("a", A("ysb", 0, S), bank(0, S))
-    store("a", "dy0", T.y[:, 0:S], A("ysb", 0, S))
-    copy("v", A("ysb", S, C), bank(1, C - S))
-    for k in range(4):
-        store("sa"[k % 2], "dos%d" % k, T.osc[4 * k:4 * k + 4, 0:C], A("sx%d" % R, 0, C, 1, 32 * k, 32 * k + 4))
-    store("s", "dy1", T.y[:, S:C], A("ysb", S, C))
-    if r > 0:
-        off = A(ll, K * (r - 1), K * r)
-        run("a", lambda: g.scalar.activation(ap(m), ap(row).indirect(ap(off)), Ident, bias=ap(mid)), [row, off, mid], [m])
-        if r > 1:
-            compose("va", "m2", "m1", beta[0], beta[1])
-            m = A("m2", 0, C)
-        emit(m)
+            sem, n = (a[0], 16) if kind in ("load", "store") else (own[e], 1)
+            call(e, kind, a).then_inc(T.sem[sem], n)
+            count[sem] += n
+            note(e, reads, writes, sem, count[sem])
     for s in SEMAPHORES:
         if count[s] > waited[s]:
             g.wait_ge(T.sem[s], count[s])

from concourse.bass import DstId, RemoteDMATransfer
from concourse.mybir import dt, AluOpType, ActivationFunctionType

C, R, N = 416, 2, 8
K, KV, KS, SLOT = C // 16, 14, 18, 32
S, MID, STEP, BIG = 16 * KS, C // 2, 2.0, 2.0 ** 40
FX, U8 = "float8_e4m3fn_x4", "uint8"
OPT = {"ychunks": ((0, 26),), "half": 5, "r0v": 6, "psplit": 2, "zero": 0, "zp": 0,
       "ahead": (0, 0), "last": ((0, 18), (18, 26)), "early": (7, 7, 7, 7, 7, 7, 7)}
ABC = "0123456789abcdefghijklmnopqrstuvwxyzABCDEFGHIJKLMNOPQRSTUVWXYZ!#$%&()*+,-./:;<=>?@[]^{|}~"
ORDER = ['4000000ggg82eokeqeem0ugkmcg0e4knmkikkkkkecjiji4eeeee6c2eiee688a8888c8888a088806660ccc8aaca8444a57764442488655646504326828a993c20082b05a6234201210406442020212000020a6042002202000000002002664200zd2u00042554a85406210463a2e34355202843b4a590020640120100030214200b6201000', '002ggi200000go0qaaacqcige68i4j68ag8eg6eej48aaa0a048666604caa886446644644464022222aaacacaa624b2782432663284267243662272222ad55242222222434220000668442222202200000000008846046642205204310214268a00122bb107202500030973504202ca42020401', '0200020e8egcgccg800iac00ec04460ec22eda8cg46466a27454440222a8666644264242422222422aaa4aca8db8442534224324844754544b44944447446d987622223342222008866486420002000000020082624042420653522d24c38490062c432604247200411330232274018807430020', '008e042acceem688co84k6i000006k6kge2deg2a248c4296786664440888866046644242224222422a8846c6866722737422401523a4862b62eae28006112090110210542050030000004084404622004002020000002624b40842202645324021cc3684384h010cc8685302550035902034201224b215075100', '00000226ce4ee4a80ge80eoikklgeg4e0046e648gccc42898a8842440224864242242642422222422a8888aa8b24246475400120a8c43542c92a3a20a0663175200010a75520003000000040802224202020020200000088662242220db6452002j1c2332222846iecbf755a242003d3007b57200406022073541131', '2200000042e28cgamcas8e8cssrscm6k8488ilgg4266cb8aaa84666eeaaa88aa6686646442222222a68b82fa86604928644652a502403c6a5a9e22e32250124072250304007332052002000000a26420042002000200000086494420ff44000220f010400141602631242a10a88601412033100009732245f70220503130', '4iii4220o4c4gg000cca4cq80r042m2288ge024660ecacac0bcaa606604a48864644448444464446022aa6b82c6862d2467446243456476445248008450928810cca8203152530304020110022120000084642422000400002000200846924844409050300046n1708aec225420k30c0003318088030120005317750202022deda22201300', '24g0e0024mg80ac8e8oeq0qocec8ckeie8c0eehac82adc846662444cca26686464242222042224222b0642235222643488456a8656502297526e882025307020523004003532030302000040864426202002000200020040920552000862l51a8c6i26233eee2202497010c0031225d5000aa1022353250098052001']

SCRATCH = {"ps": ("psum", [128, 4096], "float32"), "pri": ("sbuf", [128, K], "int32"),
           "ipi": ("sbuf", [128, 1], "int32"), "ipm": ("sbuf", [128, 1], "int32")}
for _d, _w, _names in (
        ("bfloat16", 512, "ut at sc2"), ("bfloat16", C, "a1 a2 idr vm r0 r1 r2 r3 r4 sc1 sc3 sc4"),
        ("bfloat16", 8 * C, "br"), ("bfloat16", 16, "f1 f3 f4 fa fb"), ("bfloat16", 3 * C, "sv"),
        ("bfloat16", 48, "bf"), ("bfloat16", 32, "bw"), ("bfloat16", 4 * C, "x0 x1 x2 yt0 yt1 mb"),
        (FX, 128, "qu qu2 qa"), (U8, 128, "su su2 sa"), (FX, 512, "vq wq"), (U8, 512, "vp wp"),
        (FX, C, "qx0 qx1 qx2 qy0 qy1 qz0 qz1 qp0 qp1 qr0 qr1"), (U8, C, "sx0 sx1 sx2 sy0 sy1 sz0 sz1 sq0 sq1 sr0 sr1"),
        ("float32", 1, "ipf ip16 ip17 mid e1 e2 e4"), ("float32", K, "tm"), ("float32", 32, "jb jw"),
        ("float32", 96, "uu wt tb cw"), ("float32", C, "sp sn m1 m2 ysb"), ("float32", 4 * C, "pv pw"),
        ("uint16", K, "pr16 c16 o4 oh ob o16 id16 ls0 ls1"), ("uint16", 8, "uoff"), ("uint16", 96, "ot"),
        ("uint16", 4 * K, "oy"), ("uint16", (N - 1) * SLOT, "ll0 ll1")):
    for _n in _names.split():
        SCRATCH[_n] = ("sbuf", [128, _w], _d)

SEMAPHORES = ("cv ca ct cg sent dx0 dx1 du dpr dvc dvs dwc dws da doc0 doc1 doc2 dos0 dos1 dos2 dos3 dy0 dy1 dy2 dol".split()
              + ["z%d_%d" % (t, h) for t in range(R) for h in range(3)]
              + ["l%d_%d" % (t, q) for t in range(R) for q in range(N - 1)])


def list_takers(q, t):
    head = [q + 1] + ([0] if 0 < q < N - 1 - OPT["ahead"][t] else [])
    return (head[::-1] if OPT["zero"] else head) + list(range(N - 1, q + 1, -1))


def A(name, c0, c1, step=1, p0=0, p1=128):
    return (name, c0, c1, step, p0, p1)


def cols(d):
    return (d[2] - d[1] + d[3] - 1) // d[3]


def meet(a, b):
    if a[0] == "ps":
        return a[1] // 512 == b[1] // 512
    if a[2] <= b[1] or b[2] <= a[1] or a[5] <= b[4] or b[5] <= a[4]:
        return False
    return not (a[3] == b[3] and a[3] > 1 and (a[1] - b[1]) % a[3])


def steps(r):
    out, now = [], [0]

    def put(es, kind, args, reads, writes):
        out.append((es, kind, args, reads, writes, now[0]))

    def copy(es, o, i, scale=None):
        put(es, "copy", (o, i, None, scale, None), [i], [o])

    def gather(es, o, win, off, scale=None, add=None):
        put(es, "copy", (o, win, off, scale, add), [win, off] + ([A("mid", 0, 1)] if add else []), [o])

    def compose(o, win, off, es="va", add=None, kv=KV):
        fixed = len(es) == 3
        gather("a" if fixed else es, A(o[0], o[1] + 16 * kv, o[1] + C), win, A(off[0], off[1] + kv, off[1] + K), None, add)
        if kv:
            gather("v" if fixed else es, A(o[0], o[1], o[1] + 16 * kv), win, A(off[0], off[1], off[1] + kv), None, add)

    def ts(o, i, s1, s2, op0, op1=None):
        put("v", "ts", (o, i, s1, s2, op0, op1), [i] + [s for s in (s1, s2) if isinstance(s, tuple)], [o])

    def tt(o, i0, i1, op, off=None):
        put("v", "tt", (o, i0, i1, op, off), [i0, i1] + ([off] if off else []), [o])

    def turn(o, i):
        put("v", "turn", (o, i), [i], [o])

    def scan(o, d0, d1, op0, op1):
        put("v", "scan", (o, d0, d1, op0, op1), [d0, d1], [o])

    def keep(o, d):
        scan(A(o, 0, C), A("a2", 0, C), d, "mult", "add")

    def ends(name, p0=0, p1=128, c1=C):
        return A(name, 15, c1, 16, p0, p1)

    def number(o, i):
        ts(o, i, A("e2", 0, 1, 1, i[4], i[5]), float(MID), "mult", "add")

    def quant(q, s, x, c0, c1):
        a, b, c = A(q, c0, c1), A(s, c0, c1), A(x, 4 * c0, 4 * c1)
        put("v", "quant", (a, b, c), [c], [a, b])

    def pick(q2, s2, q, s, n, off, c0=0):
        c1 = c0 + 16 * cols(off)
        put("va", "copy", (A(s2, c0, c1), A(s, 0, n), off, None, None), [A(s, 0, n), off], [A(s2, c0, c1)])
        put("v", "codes", (A(q2, c0, c1), A(q, 0, n), off), [A(q, 0, n), off], [A(q2, c0, c1)])

    def bank(k, n=C):
        return A("ps", 512 * k, 512 * k + n)

    def mm(k, wq, ws, w0, xq, xs, c0, c1):
        a = (bank(k, c1 - c0), A(wq, w0, w0 + 128), A(ws, w0, w0 + 128), A(xq, c0, c1), A(xs, c0, c1))
        put("t", "mm", a, list(a[1:]), [a[0]])

    def load(e, sem, d, name, c0=None, c1=None):
        put(e, "load", (sem, d, name, c0, c1), [], [d, A("loads", 0, 1)] if e == "s" else [d])

    def store(sem, name, where, d):
        put("sa", "store", (sem, name, where, d), [d], [])

    def fill(d, v):
        put("v", "fill", (d, v), [], [d])

    def iota(d, pattern, cm, small=True, base=0):
        put("g", "iota", (d, pattern, base, cm, small), [], [d])

    def row(name, c0=0):
        return A(name, c0, c0 + C)

    def plane(name, b, k0=0, k1=K):
        return A(name, C * b + 16 * k0, C * b + 16 * k1)

    def slot(t, q):
        return A("ll%d" % t, SLOT * q, SLOT * q + K)

    chunks = OPT["ychunks"]
    for t in range(R):
        for h, (k0, k1) in enumerate(chunks):
            put("", "lands", ("z%d_%d" % (t, h), (r - 1) % N, 2), [], [A("qz%d" % t, 16 * k0, 16 * k1), A("sz%d" % t, 16 * k0, 16 * k1)])
        for q in range(N - 1):
            if r in list_takers(q, t):
                put("", "lands", ("l%d_%d" % (t, q), q, 1), [], [slot(t, q)])

    load("a", "dpr", A("pri", 0, K), "pr")
    load("s", "du", A("ut", 0, 512), "u")
    load("s", "dx0", A("x0", 0, 4 * S), "x", 0, 4 * S)
    load("s", "dx1", A("x0", 4 * S, 4 * C), "x", 4 * S, 4 * C)
    load("s", "dvc", A("vq", 0, 512), "vc")
    load("s", "dvs", A("vp", 0, 512), "vs")
    load("s", "dwc", A("wq", 0, 512), "wc")
    load("s", "dws", A("wp", 0, 512), "ws")
    load("s", "da", A("at", 0, 512), "a")

    iota(A("ipi", 0, 1), [[0, 1]], 1, False)
    iota(A("jb", 0, 32), [[16, 32]], 0)
    iota(row("idr"), [[1, C]], 0, True, -MID)
    fill(A("cw", 3 * K, 96), 0.0)
    fill(A("tb", 0, 3 * K, 3), 0.0)
    fill(A("sv", 13, 3 * C, 16), 0.0)
    if r < N - 1:
        fill(A("sc2", C, 512), 0.0)
    fill(A("mid", 0, 1), float(MID))
    ip, ip16, ip17, e1, e2, e4 = [A(n, 0, 1) for n in ("ipf", "ip16", "ip17", "e1", "e2", "e4")]
    jb16, jw, dd, jp = A("jb", 0, 16), A("jw", 0, K), A("tb", 1, 3 * K, 3), A("tb", 2, 3 * K, 3)
    ts(A("ipm", 0, 1), A("ipi", 0, 1), 15, None, "bitwise_and")
    copy("v", A("uoff", 0, 8), A("jb", 0, 8))
    copy("v", ip, A("ipm", 0, 1))
    ts(A("jw", 0, 32), A("jb", 0, 32), ip, None, "add")
    ts(A("o16", 0, K), A("jb", 0, K), 0.0, ip, "mult", "add")
    ts(ip16, ip, 16.0, None, "mult")
    ts(ip17, ip, 16.0, 16.0, "mult", "add")
    ts(e1, ip, -STEP, 15 * STEP, "mult", "add")
    ts(e2, ip, 15.0, 1 / BIG, "is_equal", "max")
    ts(e4, e2, 4.0, None, "mult")
    ts(A("f1", 0, 16), jb16, ip16, 32 * STEP, "not_equal", "mult")
    ts(A("fa", 0, 16), A("f1", 0, 16), -31 * STEP, None, "add")
    ts(A("f3", 0, 16), jb16, ip17, BIG, "is_equal", "mult")
    ts(A("f4", 0, 16), jb16, ip16, None, "not_equal")
    tt(A("fb", 0, 16), A("f3", 0, 16), A("f4", 0, 16), "max")
    gather("a", row("a1"), A("fa", 0, 16), A("o16", 0, K))
    gather("a", row("a2"), A("fb", 0, 16), A("o16", 0, K))
    turn(A("uu", 0, 32), A("jw", 0, 32))
    turn(A("uu", 32, 64), A("jw", 0, 32))
    copy("v", A("o4", 0, K, 1, 0, 64), A("jw", 0, K, 1, 0, 64))
    many = N - 1 if r == 0 else r - 1
    halved = many >= OPT["half"]
    if halved:
        copy("v", A("oh", 0, K, 1, 0, 64), A("jw", 0, K, 1, 0, 64))
        if many % 2:
            copy("v", A("id16", 0, K), jw)
    copy("v", A("pr16", 0, K), A("pri", 0, K))
    tt(dd, A("pri", 0, K), jw, "subtract")
    quant("qu", "su", "ut", 0, 128)
    ts(A("tm", 0, K), dd, e1, None, "mult")
    pick("qu2", "su2", "qu", "su", 128, A("uoff", 0, 8))
    tt(jp, jw, A("tm", 0, K), "subtract")
    quant("qa", "sa", "at", 0, 128)

    def pieces(t):
        return OPT["last"] if t == R else ((0, KS), (KS, K))

    def state(t, h):
        c0, c1 = [16 * k for k in pieces(t)[h]]
        qx, sx = "qx%d" % t, "sx%d" % t
        quant(qx, sx, "x%d" % t, c0, c1)
        mm(4 + h, "qu2" if t < R else "qa", "su2" if t < R else "sa", 0, qx, sx, c0, c1)
        if t == R:
            store("doc%d" % h, "oc", (0, 128, 4 * c0, 4 * c1), A(qx, c0, c1))
            copy("va", A("ysb", c0, c1), bank(4 + h, c1 - c0))
            store("dy%d" % h, "y", (0, 128, c0, c1), A("ysb", c0, c1))
        elif h == 0:
            mm(6, "qu2", "su2", 0, qx, sx, c0, c1)

    state(0, 0)
    state(0, 1)
    for t in range(R):
        now[0] = t
        x, xn, yt = "x%d" % t, "x%d" % (t + 1), "yt%d" % t
        qy, sy, qz, sz, qp, sq = ["%s%d" % (n, t) for n in ("qy", "sy", "qz", "sz", "qp", "sq")]
        ls, ll = "ls%d" % t, "ll%d" % t

        copy("va", A("sp", 0, S), bank(4, S))
        copy("va", A("sn", 0, S), bank(6, S), -1.0)
        copy("va", A("sp", S, C), bank(5, C - S))
        gather("a", A("sn", S, C), row("sp"), A("pr16", KS, K), -1.0)
        tt(A("vm", 0, S), row("sp"), A("sn", 0, S), "is_gt", A("pr16", 0, KS))
        tt(A("vm", S, C), bank(5, C - S), A("sn", S, C), "is_gt")
        scan(A("sv", 0, 3 * C, 3), row("a1"), row("vm"), "add", "max")
        scan(A("cw", 0, 3 * K), A("sv", 13, 3 * C, 16), A("tb", 0, 3 * K), "mult", "add")
        copy("v", A("c16", 0, K), A("cw", 2, 3 * K, 3))

        compose(row("r0"), row("idr"), A("c16", 0, K), "fix", None, OPT["r0v"])
        turn(A("uu", 64, 96), A("cw", 2, 96, 3))
        for a in range(3):
            turn(A("uu", 32, 64, 1, 32 * a + 32, 32 * a + 64), A("cw", 2, 96, 3, 32 * a, 32 * a + 32))
        turn(A("uu", 0, 32, 1, 64, 128), A("cw", 2, 96, 3, 0, 64))
        turn(A("wt", 0, 32), A("uu", 48, 80))
        copy("v", A("ot", 0, K), A("wt", 0, K))
        turn(A("wt", 32, 64), A("uu", 32, 64))
        turn(A("wt", 64, 96), A("uu", 16, 48))
        copy("v", A("ot", 32, 96), A("wt", 32, 96))
        compose(row("r1"), row("r0"), A("ot", 0, K), "fix")
        compose(row("r2"), row("r1"), A("ot", 32, 58), "fix")
        compose(row("r3"), row("r2"), A("ot", 64, 90), "fix")
        keep("sc1", row("r3"))
        number(A("o4", 0, K, 1, 64, 128), ends("sc1", 0, 64))
        compose(row("r4"), row("r3"), A("o4", 0, K), "fix")
        keep("sc2", row("r4"))

        def tell(to):
            if to:
                put("g", "list", ("l%d_%d" % (t, r), A(ls, 0, K), slot(t, r), to), [A(ls, 0, K)], [A("sends", 0, 1)])

        for k in range(4):
            ts(A("oy", K * k, K * k + K), ends("sc2"), e4, float(4 * MID + k), "mult", "add")
        if r < N - 1:
            turn(A("bf", 0, 32, 1, 96, 128), ends("sc2", 96, 128, 512))
            copy("v", A("bf", 32, 48, 1, 96, 128), A("bf", 16, 32, 1, 96, 128))
            turn(A("bw", 0, 32, 1, 96, 128), A("bf", 16, 48, 1, 96, 128))
            for a in range(4):
                number(A(ls, 0, K, 1, 32 * a, 32 * a + 32), A("bw", 0, K, 1, 96, 128))
            tell(list_takers(r, t)[:OPT["early"][r]])
        for h, (k0, k1) in enumerate(chunks):
            for k in range(4):
                for a, b in ((k0, KV), (KV, k1)) if k < OPT["psplit"] and len(chunks) == 1 else ((k0, k1),):
                    gather("va", A(yt, 64 * a + k, 64 * b, 4), A(x, 0, 4 * C), A("oy", K * k + a, K * k + b))
            c0, c1 = 16 * k0, 16 * k1
            quant(qy, sy, yt, c0, c1)
            if r and h == len(chunks) - 1:
                pick(qp, sq, qy, sy, C, slot(t, r - 1))
            for a, b in ((qz, qy), (sz, sy)) if r < N - 1 or not OPT["ahead"][t] else ((qz, qp), (sz, sq)):
                put("g", "send", ("z%d_%d" % (t, h), A(a, c0, c1), A(b, c0, c1)), [A(b, c0, c1)], [A("sends", 0, 1)])
        if r < N - 1:
            tell(list_takers(r, t)[OPT["early"][r]:])

        if r == 0:
            lists = [(ll, SLOT * q) for q in range(N - 2 - OPT["ahead"][t], 0, -1)] + [(ls, 0)]
        else:
            lists = [(ll, SLOT * q) for q in range(r - 2, -1, -1)]
        if len(lists) > 1:
            n = (len(lists) + 1) // 2 if halved else len(lists)
            inner = [("id16", 0)] * (2 * n - len(lists)) + lists[n:]
            for i in range(n):
                name, k0 = lists[i]
                if halved:
                    copy("v", A(name, k0, k0 + K, 1, 0, 64), A(inner[i][0], inner[i][1], inner[i][1] + K, 1, 0, 64))
                compose(row("br", C * i), row("br", C * i - C) if i else row("idr"), A(name, k0, k0 + K))
            if halved:
                keep("sc4", row("br", C * n - C))
                number(A("oh", 0, K, 1, 64, 128), ends("sc4", 0, 64))
                compose(row("br", C * n), row("br", C * n - C), A("oh", 0, K))
                keep("sc3", row("br", C * n))
                for p in (0, 64):
                    number(A("ob", 0, K, 1, p, p + 64), ends("sc3", 64, 128))
            else:
                keep("sc3", row("br", C * n - C))
                number(A("ob", 0, K), ends("sc3"))
        beta = (ll, 0) if r == 2 else ("ob", 0)

        def off(k0, k1):
            return A(beta[0], beta[1] + k0, beta[1] + k1)

        def wbank(b, h):
            return b if h % 2 else 4 + b

        def scaled(k0, k1):
            km = (k0 + k1) // 2
            for a, b in ((k0, km), (km, k1)):
                copy("va", A(xn, 64 * a, 64 * b), A("mb", 64 * a, 64 * b), 0.03125)

        if r == 0 and OPT["zp"]:
            for b in range(4):
                mm(b, "vq", "vp", 128 * b, qy, sy, 0, C)
                copy("va", plane("pv", b), bank(b))
            for h, (k0, k1) in enumerate(pieces(t + 1)):
                pick("qr%d" % t, "sr%d" % t, qz, sz, C, off(k0, k1), 16 * k0)
                for b in range(4):
                    mm(wbank(b, h), "wq", "wp", 128 * b, "qr%d" % t, "sr%d" % t, 16 * k0, 16 * k1)
                    tt(A("mb", 64 * k0 + b, 64 * k1, 4), bank(wbank(b, h), 16 * (k1 - k0)), plane("pv", b, k0, k1), "max")
                scaled(k0, k1)
                state(t + 1, h)
            continue
        if r == 0:
            for b in range(4):
                mm(b, "vq", "vp", 128 * b, qy, sy, 0, C)
                copy("va", plane("pv", b), bank(b), 0.03125)
            for h, (k0, k1) in enumerate(chunks):
                for b in range(4):
                    mm(wbank(b, h), "wq", "wp", 128 * b, qz, sz, 16 * k0, 16 * k1)
                    copy("va", plane("pw", b, k0, k1), bank(wbank(b, h), 16 * (k1 - k0)), 0.03125)

            def place(b, k0, k1):
                tt(A(xn, 64 * k0 + b, 64 * k1, 4), plane("pw", b), plane("pv", b, k0, k1), "max", off(k0, k1))
        else:
            for b in range(4):
                mm(b, "vq", "vp", 128 * b, qp, sq, 0, C)
                copy("va", plane("pv", b), bank(b))
            for h, (k0, k1) in enumerate(chunks):
                for b in range(4):
                    mm(wbank(b, h), "wq", "wp", 128 * b, qz, sz, 16 * k0, 16 * k1)
                    tt(plane("pw", b, k0, k1), bank(wbank(b, h), 16 * (k1 - k0)), plane("pv", b, k0, k1), "max")

            def place(b, k0, k1):
                o = A(xn, 64 * k0 + b, 64 * k1, 4)
                if r == 1:
                    copy("va", o, plane("pw", b, k0, k1), 0.03125)
                else:
                    gather("va", o, plane("pw", b), off(k0, k1), 0.03125)

        for h, (k0, k1) in enumerate(pieces(t + 1)):
            for b in (3, 2, 1, 0):
                place(b, k0, k1)
            state(t + 1, h)

    m = row("m1")
    if r == 0:
        put("va", "copy", (m, row("r4"), None, None, float(MID)), [row("r4"), A("mid", 0, 1)], [m])
    else:
        compose(m, row("r4"), slot(R - 1, r - 1), "va", float(MID))
        if r > 1:
            compose(row("m2"), m, off(0, K))
            m = row("m2")
    store("dol", "ol", (0, 8, 0, C), m)
    for k in range(4):
        store("dos%d" % k, "osc", (4 * k, 4 * k + 4, 0, C), A("sx%d" % R, 0, C, 1, 32 * k, 32 * k + 4))
    return out


def needs(every):
    seen, out = {}, []
    for i, st in enumerate(every):
        mine = [(d, False) for d in st[3]] + [(d, True) for d in st[4]]
        need, true = set(), set()
        for d, w in mine:
            for o, ow, j in seen.get(d[0], []):
                if (w or ow or d[0] == "ps") and meet(d, o):
                    need.add(j)
                    if ow and not w:
                        true.add(j)
        for d, w in mine:
            seen.setdefault(d[0], []).append((d, w, i))
        out.append((need, true))
    return out


def ordered(every, word):
    before = [n for n, _ in needs(every)]
    done = set(i for i, st in enumerate(every) if st[1] == "lands")
    out = []
    for k in range(len(every) - len(done)):
        ready = [i for i in range(len(every)) if i not in done and before[i] <= done]
        x = ABC.index(word[k]) if word else 0
        out.append((ready[x // 2], every[ready[x // 2]][0][x % 2]))
        done.add(ready[x // 2])
    return out


def rank_program(g, core, T, topo):
    r = T.rank_of(core)
    if r is None:
        return
    every = steps(r)
    Op = {"add": AluOpType.add, "subtract": AluOpType.subtract, "mult": AluOpType.mult, "max": AluOpType.max,
          "is_gt": AluOpType.is_gt, "is_equal": AluOpType.is_equal, "not_equal": AluOpType.not_equal,
          "bitwise_and": AluOpType.bitwise_and}
    Copy, Ident = ActivationFunctionType.Copy, ActivationFunctionType.Identity
    queue = {"v": g.vector, "a": g.scalar, "t": g.tensor, "g": g, "s": g.sync}
    own = {"v": "cv", "a": "ca", "t": "ct", "g": "cg"}
    count = {s: 0 for s in SEMAPHORES}
    waited = {s: 0 for s in SEMAPHORES}
    clock = {e: {} for e in queue}
    log = {}

    def ap(d):
        if d[3] == 1:
            return T[d[0]][d[4]:d[5], d[1]:d[2]]
        return T[d[0]][d[4]:d[5], d[1]:d[2]:d[3]]

    def raw(d):
        return ap(d).bitcast(dt.uint8) if SCRATCH[d[0]][2] == FX else ap(d)

    def order(e, reads, writes):
        need = {}
        for d, w in [(d, False) for d in reads] + [(d, True) for d in writes]:
            for (o, ow, oe, sem, val, seen) in log.get(d[0], []):
                if (w or ow or (d[0] == "ps" and oe != e)) and meet(d, o):
                    if sem not in need or need[sem][0] < val:
                        need[sem] = (val, seen)
        for sem, (val, seen) in sorted(need.items(), key=lambda kv: -len(kv[1][1])):
            if clock[e].get(sem, 0) < val:
                queue[e].wait_ge(T.sem[sem], val)
                waited[sem] = max(waited[sem], val)
                for s, v in seen.items():
                    clock[e][s] = max(clock[e].get(s, 0), v)

    def note(e, reads, writes, sem, val):
        seen = dict(clock[e]) if e else {}
        seen[sem] = val
        for d, w in [(d, False) for d in reads] + [(d, True) for d in writes]:
            log.setdefault(d[0], []).append((d, w, e, sem, val, seen))

    def call(e, kind, a):
        v = g.vector
        if kind == "copy":
            o, i, off, scale, add = a
            src = ap(i).indirect(ap(off)) if off else ap(i)
            if e == "a":
                if add:
                    return g.scalar.activation(ap(o), src, Ident, bias=ap(A("mid", 0, 1)))
                if scale:
                    return g.scalar.activation(ap(o), src, Copy, scale=scale)
                return g.scalar.activation(ap(o), src, Copy)
            if add or scale:
                return v.tensor_scalar(ap(o), src, add or scale, None, Op["add" if add else "mult"])
            return v.tensor_copy(ap(o), src)
        if kind == "codes":
            return v.tensor_copy(ap(a[0]).bitcast(dt.uint32), ap(a[1]).bitcast(dt.uint32).indirect(ap(a[2])))
        if kind == "ts":
            v1, v2 = [ap(s) if isinstance(s, tuple) else s for s in a[2:4]]
            if a[5] is None:
                return v.tensor_scalar(ap(a[0]), ap(a[1]), v1, None, Op[a[4]])
            return v.tensor_scalar(ap(a[0]), ap(a[1]), v1, v2, Op[a[4]], Op[a[5]])
        if kind == "tt":
            return v.tensor_tensor(ap(a[0]), ap(a[1]).indirect(ap(a[4])) if a[4] else ap(a[1]), ap(a[2]), Op[a[3]])
        if kind == "turn":
            return v.transpose(ap(a[0]), ap(a[1]))
        if kind == "scan":
            return v.tensor_tensor_scan(ap(a[0]), ap(a[1]), ap(a[2]), 0.0, Op[a[3]], Op[a[4]])
        if kind == "quant":
            return v.quantize_mx(ap(a[0]), ap(a[1]), ap(a[2]))
        if kind == "mm":
            return g.tensor.matmul_mx(ap(a[0]), ap(a[1]), ap(a[2]), ap(a[3]), ap(a[4]), True, True)
        if kind == "fill":
            return v.memset(ap(a[0]), a[1])
        if kind == "iota":
            if a[4]:
                return g.iota(ap(a[0]), a[1], a[2], a[3], allow_small_or_imprecise_dtypes=True)
            return g.iota(ap(a[0]), a[1], a[2], a[3])
        if kind == "load":
            return queue[e].dma_start(raw(a[1]), T[a[2]][:] if a[3] is None else T[a[2]][:, a[3]:a[4]])
        p0, p1, c0, c1 = a[2]
        if a[1] == "ol":
            return queue[e].dma_start(T.ol[:], T[a[3][0]][0:128:16, 0:C])
        return queue[e].dma_start(T[a[1]][p0:p1, c0:c1], raw(a[3]))

    nxt = T.cores[(r + 1) % N]
    for _, kind, a, _, writes, _ in every:
        if kind == "lands":
            count[a[0]] = a[2] * len(topo.engines(T.cores[a[1]], core))
            note(None, [], writes, a[0], count[a[0]])

    for i, e in ordered(every, ORDER[r] if ORDER else None):
        _, kind, a, reads, writes, _ = every[i]
        order(e, reads, [d for d in writes if d[0] in SCRATCH])
        if kind == "list":
            to = [topo.addr(T.cores[q]) for q in a[3]]
            g.remote_dma_fused([RemoteDMATransfer(dst_ids=[DstId(rid=x[0], pnc=x[1]) for x in to],
                                                  dma_engine_mask=topo.mask(core, nxt), remote_sem=T.sem[a[0]],
                                                  srcs=[ap(a[1])], dsts=[ap(a[2]) for _ in to])], local_sem=T.sem.sent)
            count["sent"] += len(topo.engines(core, nxt))
        elif kind == "send":
            rid, pid, _ = topo.addr(nxt)
            g.remote_dma(raw(a[1]), raw(a[2]), T.sem[a[0]], T.sem.sent, pid, rid, topo.mask(core, nxt))
            count["sent"] += len(topo.engines(core, nxt))
        else:
            sem, n = (a[0], 16) if kind in ("load", "store") else (own[e], 1)
            call(e, kind, a).then_inc(T.sem[sem], n)
            count[sem] += n
            note(e, reads, writes, sem, count[sem])
    for s in SEMAPHORES:
        if count[s] > waited[s]:
            g.wait_ge(T.sem[s], count[s])
